import numpy as np, ml_dtypes
CORES = [35,38,43,46]
N = 4
BF = ml_dtypes.bfloat16
W, L, S, T, HS, AS = 4096, 256, 16, 3, 1, 2
def parts(rng):
    D = rng.integers(0, W, (N, 8, 16, W)); one = rng.integers(0, W, (N, 8, 1, W))
    D = np.where((rng.random((N, 8, 1, W)) < 0.5) & (rng.random(D.shape) < 0.5), one, D)
    D = np.where(rng.random(D.shape) < 0.25, S * rng.integers(0, L, D.shape) + rng.integers(0, T, D.shape), D)
    X = rng.integers(0, 256, (N, 8, 16, W)); th = rng.integers(1000, 1800, (N, 8, 16))
    n = np.array([1, 1, 2, 2, 4, 4, 16, 16])[np.argsort(rng.random((N, 8)), axis=1)]
    j = (np.arange(16)[None, None, :] % n[:, :, None])[..., None]
    ti = np.take_along_axis(np.argsort(rng.random((N, 8, 16, 16)), axis=-1)[..., :3], j, 2)
    sg = np.take_along_axis(2 * rng.integers(0, 2, (N, 8, 16, 3)) - 1, j, 2)
    return D, X, th, ti, sg
def pack(D, X, th, ti, sg):
    return {"dg": np.ascontiguousarray(D.reshape(N, 128, W)).astype(np.int32), "xv": np.ascontiguousarray(X.reshape(N, 128, W)).astype(np.float32).astype(BF),
            "th": np.ascontiguousarray(th.reshape(N, 128, 1)).astype(np.int32), "ti": np.ascontiguousarray(ti.reshape(N, 128, 3)).astype(np.int32), "sg": np.ascontiguousarray(sg.reshape(N, 128, 3)).astype(np.int32)}
def setup_inputs(rng):
    return pack(*parts(rng))
def setup_inputs_corners(rng):
    D, X, th, ti, sg = parts(rng); c = np.arange(W)[None, :]; base = int(rng.integers(0, N)); o = rng.permutation(8)
    th = rng.choice(np.array([0, 1, 1365, 4080, 4081, 4081]), th.shape)
    for q in range(N):
        for g in range(8):
            m = int(o[g])
            if m == 0: D[q, g] = c
            if m == 1: D[q, g] = rng.choice(np.array([0, W - 1]), (16, W))
            if m == 2: D[q, g] = (c + 1 + np.arange(16)[:, None]) % W; th[q, g] = 4081
            if m == 3: D[q, g] = S * rng.integers(0, L, (16, W)) + rng.integers(0, T, (16, W))
            if m == 4: D[q, g] = rng.integers(0, W, (1, W)); th[q, g] = 4081
            if m == 5: D[q, g] = (c - 1) % W; th[q, g] = 0
            if m == 6: D[q, g] = rng.integers(0, W // 2, (16, W)) + (W // 2) * int(rng.integers(0, 2)); th[q, g] = 4081
            if m == 7: th[q, g] = 4080
    k = rng.random((N, 8, 1, W)); X = np.where(k < 0.1, 0, np.where(k < 0.2, 255, X))
    for q in (base % N, (base + 1) % N):
        for t in range(T): X[q, :, :, t::S] = 255
    a = (base + 2) % N; b = (base + 3) % N
    sg[a, :, :, 0] = -sg[a, :, :, 1]; sg[b] = sg[b][:, :, :1]
    return pack(D, X, th, ti, sg)
def setup_inputs_ties(rng):
    D, X, th, ti, sg = parts(rng)
    pr = rng.integers(0, 256, (8, 16, 24))
    pr[..., 12:] = np.minimum(pr[..., :12] + (np.arange(16)[None, :, None] == rng.integers(0, 16, (8, 1, 12))), 255)
    X = np.take_along_axis(np.broadcast_to(pr, (N, 8, 16, 24)), rng.integers(0, 24, (N, 8, 1, W)), 3)
    dd = np.add.reduce(np.abs(pr[:, :, :, None] - pr[:, :, None, :]), axis=1)
    th = dd[np.arange(8)[None, :, None], rng.integers(0, 24, (N, 8, 16)), rng.integers(0, 24, (N, 8, 16))] + rng.integers(0, 2, (N, 8, 16))
    return pack(D, X, th, ti, sg)
def setup_inputs_spread(rng):
    D, X, th, ti, sg = parts(rng)
    X = np.minimum((np.exp2(8 * rng.random((N, 8, 1, W))) * rng.random(X.shape)).astype(np.int64), 255)
    e = rng.choice(np.array([1, 2, 4]), (N, 8, 16, 1)); u = rng.random(D.shape)
    D = np.minimum((W * np.where(e == 1, u, np.where(e == 2, u * u, u * u * u * u))).astype(np.int64), W - 1)
    D = np.where(rng.random((N, 8, 16, 1)) < 0.5, D, W - 1 - D)
    th = np.minimum(np.exp2(12 * rng.random(th.shape)).astype(np.int64), 4081)
    return pack(D, X, th, ti, sg)
def setup_inputs_ends(rng):
    D, X, th, ti, sg = parts(rng)
    k = rng.random((N, 8, 1, W)); D = np.where(k < 0.4, (W - 1) * rng.integers(0, 2, k.shape), np.where(k < 0.75, (W - 1) * rng.integers(0, 2, D.shape), D))
    k = rng.random((N, 8, 1, W)); X = 255 * np.where(k < 0.3, rng.integers(0, 2, k.shape), rng.integers(0, 2, X.shape))
    th = 4081 * rng.integers(0, 2, th.shape); th[:, 0, 0] = 0; th[:, 7, 15] = 4081
    low = np.zeros((N, 8, 16, 1), np.int64); mid = rng.integers(1, 15, (N, 8, 16, 1))
    low[:, 4] = 1; mid[:, 4] = rng.integers(2, 15, (N, 16, 1))
    mid[:, 7] = 1 + np.arange(16).reshape(16, 1) % 14
    ti = np.concatenate([low, np.full((N, 8, 16, 1), 15), mid], axis=-1)
    ti = np.take_along_axis(ti, np.argsort(rng.random(ti.shape), axis=-1), 3)
    for q in (N - 2, N - 1, 0):
        c = (W - 1) * rng.integers(0, 2, (8, 1, L)); z = 255 * rng.integers(0, 2, (8, 1, L))
        c[..., 0] = 0; c[..., 1] = W - 1; c[..., L - 1] = W - 1; z[..., 0] = 0; z[..., 1] = 0; z[..., L - 1] = 0
        far = ((c == 0) == (z == 255)) & (rng.random((8, 1, L)) < 0.5); far[..., 0] = False; far[..., L - 1] = False
        off = (rng.integers(0, 16, (8, 16, L)) >> (3 * rng.integers(0, 2, (8, 1, L)))) * far
        x = np.abs(z - off)
        if q == N - 2:
            u = rng.permutation(8 * (L - 2))[:19 + 2 * int(rng.integers(0, 50))]; a = u // (L - 2); i = 1 + u % (L - 2)
            h = 255 * rng.integers(0, 2, (len(u), 16)); h[:, :2] = 0; h[:, 15] = 255
            c[a, 0, i] = W - 1; x[a, :, i] = h
        D[q, :, :, 0::S] = c; X[q, :, :, 0::S] = x
    for q in (N - 2, N - 1, 0, 1):
        D[q, :, :, 0] = 0; D[q, :, :, W - 1] = W - 1; X[q, :, :, 0] = 0; X[q, :, :, W - 1] = 255
    for q in (N - 1, 0):
        sg[q] = sg[q][:, :, :1]; sg[q, :, 0] = 1; sg[q, :, 15] = -1
    sg[1, :, :, 0] = -sg[1, :, :, 1]
    return pack(D, X, th, ti, sg)
def check_inputs(d):
    bad = []
    for k, lo, hi in (("dg", 0, W - 1), ("xv", 0, 255), ("th", 0, 4081), ("ti", 0, 15), ("sg", -1, 1)):
        a = np.asarray(d[k]).astype(np.float64)
        if not (np.min(a) >= lo and np.max(a) <= hi): bad.append("range of " + k)
    a = np.asarray(d["xv"]).astype(np.float64)
    if not np.all(a == np.floor(a)): bad.append("whole numbers in xv")
    a = np.asarray(d["ti"])
    if np.any(a[..., 0] == a[..., 1]) or np.any(a[..., 0] == a[..., 2]) or np.any(a[..., 1] == a[..., 2]): bad.append("different rows in a triple of ti")
    if np.any(np.asarray(d["sg"]) == 0): bad.append("no zero in sg")
    return bad
def reference(dg, xv, th, ti, sg):
    D = dg.astype(np.int64).reshape(N, 8, 16, W); X = xv.astype(np.float32).astype(np.int32).reshape(N, 8, 16, W); H = th.astype(np.int64).reshape(N, 8, 16, 1)
    G = np.zeros((N, 8, 16, 16), np.int64); np.put_along_axis(G, ti.astype(np.int64).reshape(N, 8, 16, 3), sg.astype(np.int64).reshape(N, 8, 16, 3), 3)
    def dist(q, E, x):
        y = np.take_along_axis(X[q], E.reshape(8, 1, 16 * L), 2).reshape(8, 16, 16, L)
        return np.add.reduce(np.abs(y - x[:, :, None, :]), axis=1).astype(np.int64)
    for t in range(T):
        v = S * np.arange(L) + t; new = np.array(D); last = []
        for r in range(N):
            s = (r + 1 + t) % N; x = X[r][:, :, v]; E = D[r][:, :, v]; go = np.ones((8, 16, L), bool)
            for step in range(HS + AS):
                q = r if step < HS else s
                n = np.take_along_axis(D[q], E, 2)
                go = go & (dist(q, n, x) < H[q]); E = np.where(go, n, E)
            d = dist(s, E, x); b = np.where(np.take_along_axis(X[s], E, 2) > x, 1, -1)
            cyc = np.abs(np.matmul(G[s], b)) == 3
            charged = np.matmul(np.abs(G[s]).transpose(0, 2, 1), cyc.astype(np.int64)) > 0
            A = int(np.count_nonzero(np.any(cyc, axis=1)))
            keep = np.argmin(np.where(charged, d, 2 ** 20), axis=1)
            gone = charged & (np.arange(16)[None, :, None] != keep[:, None, :])
            new[r][:, :, v] = np.where(gone, (37 * E + d + A) & (W - 1), D[r][:, :, v]); last.append(E)
        D = new
    yd = np.concatenate([D[:, :, :, t::S] for t in range(T)], axis=3)
    return {"yd": yd.reshape(N, 128, T * L).astype(np.float32), "ye": np.stack(last).reshape(N, 128, L).astype(np.float32)}

@@ -1,0 +1,481 @@
+from concourse.bass import DstId, RemoteDMATransfer
+from concourse.mybir import AluOpType as A, AxisListType, ActivationFunctionType as F
+
+SIZES = [64, 64, 64, 64]
+CH = [(sum(SIZES[:i]), n) for i, n in enumerate(SIZES)]
+NC = len(CH)
+R = 3
+ENG2, ENG3, ENG4 = "SSSV", "VVSS", "VVVV"
+WG, RG = [2, 1, 1], [2, 2]
+BIAS = [2.0]
+RK = ["V", "V", "V"]
+SCRATCH = {
+    "dt": ("sbuf", [128, 4096], "int32"), "xt": ("sbuf", [128, 16384], "bfloat16"),
+    "thi": ("sbuf", [128, 1], "int32"), "tii": ("sbuf", [128, 3], "int32"), "sgi": ("sbuf", [128, 3], "int32"),
+    "thf": ("sbuf", [128, 1], "float32"), "thb": ("sbuf", [128, 1], "float32"), "tif": ("sbuf", [128, 3], "float32"), "sgf": ("sbuf", [128, 3], "float32"),
+    "pi": ("sbuf", [128, 1], "int32"), "pm": ("sbuf", [128, 1], "int32"), "pf": ("sbuf", [128, 1], "float32"),
+    "pmf": ("sbuf", [128, 1], "float32"), "vb": ("sbuf", [128, 1], "float32"), "bse": ("sbuf", [128, 1], "float32"),
+    "one": ("sbuf", [128, 128], "bfloat16"), "ob0": ("sbuf", [128, 128], "bfloat16"), "ob": ("sbuf", [128, 144], "bfloat16"), "ob2": ("sbuf", [128, 144], "bfloat16"), "obn": ("sbuf", [128, 144], "bfloat16"),
+    "one32": ("sbuf", [128, 128], "float32"), "idb": ("sbuf", [128, 128], "bfloat16"), "i32": ("sbuf", [128, 128], "float32"),
+    "ni32": ("sbuf", [128, 128], "float32"), "i592": ("sbuf", [128, 128], "float32"), "i16": ("sbuf", [128, 128], "float32"),
+    "ni16": ("sbuf", [128, 128], "float32"), "dg16": ("sbuf", [128, 2048], "bfloat16"), "ex": ("sbuf", [8, 128], "float32"),
+    "rs": ("sbuf", [128, 128], "float32"), "o16": ("sbuf", [8, 128], "float32"),
+    "iom": ("sbuf", [128, 128], "float32"), "gk": ("sbuf", [128, 384], "float32"), "gs1": ("sbuf", [128, 128], "float32"),
+    "gj": ("sbuf", [128, 128], "bfloat16"), "ga": ("sbuf", [128, 128], "bfloat16"), "nga": ("sbuf", [128, 128], "bfloat16"),
+    "gt": ("sbuf", [128, 128], "bfloat16"),
+    "le": ("sbuf", [128, 768], "uint16"), "eb": ("sbuf", [128, 768], "float32"), "xn": ("sbuf", [128, 768], "bfloat16"),
+    "xc": ("sbuf", [128, 768], "bfloat16"), "ec": ("sbuf", [128, 768], "float32"), "xr": ("sbuf", [128, 8192], "bfloat16"),
+    "l1": ("sbuf", [128, 768], "uint16"), "ll1": ("sbuf", [128, 768], "uint16"),
+    "r1": ("sbuf", [128, 768], "bfloat16"), "lr1": ("sbuf", [128, 768], "bfloat16"),
+    "l2": ("sbuf", [128, 256], "uint16"), "l3": ("sbuf", [128, 256], "uint16"), "l4": ("sbuf", [128, 256], "uint16"),
+    "g0": ("sbuf", [128, 4096], "float16"), "g1": ("sbuf", [128, 4096], "float16"), "g2": ("sbuf", [128, 4096], "float16"),
+    "y1": ("sbuf", [128, 4096], "bfloat16"), "y2": ("sbuf", [128, 4096], "bfloat16"), "y3": ("sbuf", [128, 4096], "bfloat16"),
+    "y4": ("sbuf", [128, 4096], "bfloat16"),
+    "b1": ("sbuf", [128, 4096], "bfloat16"), "b2": ("sbuf", [128, 4096], "bfloat16"), "b3": ("sbuf", [128, 4096], "bfloat16"),
+    "b4": ("sbuf", [128, 4096], "bfloat16"),
+    "nk": ("sbuf", [128, 1024], "float32"), "r4": ("sbuf", [128, 1024], "bfloat16"), "es": ("sbuf", [128, 1024], "float32"),
+    "ei": ("sbuf", [128, 256], "int32"), "ef": ("sbuf", [128, 256], "int32"), "val": ("sbuf", [128, 256], "float32"),
+    "bb": ("sbuf", [128, 256], "bfloat16"), "sq": ("sbuf", [128, 256], "bfloat16"), "key": ("sbuf", [128, 256], "float32"),
+    "ks": ("sbuf", [128, 128 * NC], "float32"), "mx": ("sbuf", [8, 256], "float32"), "lt": ("sbuf", [128, 256], "bfloat16"),
+    "cm": ("sbuf", [8, 256], "bfloat16"), "cn": ("sbuf", [8, NC], "float32"),
+    "gu": ("sbuf", [128, 256], "float32"), "gaa": ("sbuf", [128, 256], "float32"),
+    "qg": ("sbuf", [128, 1560], "float32"), "ql": ("sbuf", [128, 1560], "float32"),
+    "wf": ("sbuf", [128, 256], "int32"), "ydf": ("sbuf", [128, 768], "float32"), "yef": ("sbuf", [128, 256], "float32"),
+    "yel": ("sbuf", [128, 256], "float32"),
+}
+for _i in range(8):
+    SCRATCH["ps%d" % _i] = ("psum", [128, 512], "float32")
+SEMAPHORES = ["cv", "cs", "cp", "cg", "ls", "aye"]
+SEMAPHORES += ["d%d" % i for i in range(14)]
+for _t in range(R):
+    SEMAPHORES += ["ax%d" % _t, "ae%d" % _t] + ["aw%d_%d" % (_t, _c) for _c in range(NC)]
+    SEMAPHORES += ["al%d_%d" % (_t, _c) for _c in range(NC)] + ["ar%d_%d" % (_t, _c) for _c in range(NC)]
+SEMOF = {"V": "cv", "S": "cs", "P": "cp", "G": "cg"}
+CY, GA, VF, SF, PC, HOP, CALL = 0.00095, 1.5, 0.06, 0.07, 0.00048, 2.2, 0.8
+
+
+def rank_program(g, core, T, topo):
+    me = T.rank_of(core)
+    if me is None:
+        return
+    tasks, lastw, readers, tiles, sends, dmas, cur = [], {}, {}, [], [0], [0], [0.0]
+
+    def add(eng, dur, fn, rd=(), wr=(), tl=(), after=(), lag=0.0):
+        i = len(tasks)
+        deps = set(after)
+        for k in rd:
+            if k in lastw:
+                deps.add(lastw[k])
+        for k in wr:
+            if k in lastw:
+                deps.add(lastw[k])
+            deps |= readers.get(k, set())
+        for q in tl:
+            u = tiles[q]["users"]
+            j = len(u) - 1
+            while j >= 0 and tasks[u[j]]["eng"] == eng:
+                j -= 1
+            if j >= 0:
+                e = tasks[u[j]]["eng"]
+                while j >= 0 and tasks[u[j]]["eng"] == e:
+                    deps.add(u[j])
+                    j -= 1
+            u.append(i)
+        for k in rd:
+            readers.setdefault(k, set()).add(i)
+        for k in wr:
+            lastw[k] = i
+            readers[k] = set()
+        deps.discard(i)
+        tasks.append({"eng": eng, "dur": dur, "fn": fn, "deps": deps, "tl": list(tl), "lag": lag, "bias": cur[0]})
+        return i
+
+    def chunk(c):
+        cur[0] = BIAS[0] * (NC - 1 - c)
+        return CH[c]
+
+    def tile():
+        tiles.append({"users": [], "bank": -1})
+        return len(tiles) - 1
+
+    def pslice(q, a, n, P=128):
+        return T["ps%d" % tiles[q]["bank"]][0:P, a:a + n]
+
+    def V(n, fn, rd=(), wr=(), tl=()):
+        return add("V", VF + CY * max(n, 64), fn, rd, wr, tl)
+
+    def S(n, fn, rd=(), wr=(), tl=()):
+        return add("S", SF + CY * max(n, 64), fn, rd, wr, tl)
+
+    def P(n, fn, rd=(), wr=(), tl=()):
+        return add("P", PC * n, fn, rd, wr, tl)
+
+    def gq(n, fn, rd=(), wr=()):
+        return add("G", 0.19 + 2 * CY * n, fn, rd, wr)
+
+    def load(eng, fn, dur, rd=(), wr=()):
+        k = dmas[0]
+        dmas[0] += 1
+        i = add("DMA" + eng, 0.1, fn, rd, (), ())
+        tasks[i]["sem"] = "d%d" % k
+        j = add("R", 0.0, None, (), wr, (), after=(i,), lag=dur)
+        tasks[j]["wait"] = ("d%d" % k, 16)
+
+    def send(dst, src_key, out, in_, rsem, land_key):
+        es = topo.engines(core, dst)[0:8]
+        rid, pid, _ = topo.addr(dst)
+        sends[0] += len(es)
+
+        def fn():
+            g.remote_dma(out, in_, T.sem[rsem], T.sem.ls, pid, rid, sum(1 << e for e in es))
+            return []
+        i = add("G", CALL, fn, src_key, (), ())
+        j = add("R", 0.0, None, (), land_key, (), after=(i,), lag=HOP)
+        tasks[j]["wait"] = (rsem, len(es))
+
+    mm = g.tensor.matmul
+    vc, vt, vs = g.vector.tensor_copy, g.vector.tensor_tensor, g.vector.tensor_scalar
+    scan = g.vector.tensor_tensor_scan
+    act = g.scalar.activation
+
+    load("Y", lambda: g.sync.dma_start(T.dt[:], T.dg[:]), 9.0, (), ("D",))
+    load("Y", lambda: g.sync.dma_start(T.xt[:, 0:4096], T.xv[:]), 12.0, (), ("X",))
+    load("S", lambda: g.scalar.dma_start(T.tii[:], T.ti[:]), 2.0, (), ("tii",))
+    load("S", lambda: g.scalar.dma_start(T.sgi[:], T.sg[:]), 2.0, (), ("sgi",))
+    load("S", lambda: g.scalar.dma_start(T.thi[:], T.th[:]), 2.0, (), ("thi",))
+    for k in range(1, 4):
+        load("Y", lambda k=k: g.sync.dma_start(T.xt[:, 4096 * k:4096 * k + 4096], T.xt[:, 0:4096]), 4.0, ("X",), (("X4", k),))
+
+    V(64, lambda: [g.vector.memset(T.one[:], 1.0)], (), ("one",))
+    V(128, lambda: [g.vector.memset(T.one32[:], 1.0)], (), ("one32",))
+    V(64, lambda: [g.vector.memset(T.ob[:], 0.0)], (), ("ob",))
+    V(64, lambda: [g.vector.memset(T.o16[:], 16.0)], (), ("o16",))
+    V(128, lambda: [g.vector.memset(T.rs[:], 1.0)], (), ("rs",))
+    V(64, lambda: [g.vector.memset(T.rs[:, 0:128:16], 0.0)], (), ("rs",))
+    V(1024, lambda: [g.vector.memset(T.dg16[:], 0.0)], (), ("dg16",))
+    V(512, lambda: [g.vector.memset(T.r4[:], 0.0)], (), [("r4", c, k) for c in range(NC) for k in range(4)])
+    gq(128, lambda: [g.affine_select(T.idb[:], T.one[:], [[-1, 128]], A.is_equal, 0.0, 0, 1)], ("one",), ("idb",))
+    gq(128, lambda: [g.affine_select(T.ob0[:], T.one[:], [[0, 8], [1, 16]], A.is_equal, 0.0, 0, 0)], ("one",), ("ob0",))
+    gq(128, lambda: [g.affine_select(T.ob0[:], T.ob0[:], [[-16, 8], [0, 16]], A.is_ge, 0.0, 0, 1)], ("ob0",), ("ob0",))
+    gq(128, lambda: [g.affine_select(T.ob0[:], T.ob0[:], [[16, 8], [0, 16]], A.is_ge, 0.0, 15, -1)], ("ob0",), ("ob0",))
+    gq(128, lambda: [g.affine_select(T.i32[:], T.one32[:], [[-1, 128]], A.is_equal, 0.0, 0, 1)], ("one32",), ("i32",))
+    gq(128, lambda: [g.affine_select(T.ex[:], T.one32[0:8, :], [[-1, 8], [0, 16]], A.is_equal, 0.0, 0, 1)], ("one32",), ("ex",))
+    gq(1, lambda: [g.iota(T.pi[:], [[1, 1]], 0, 1)], (), ("pi",))
+    gq(128, lambda: [g.iota(T.iom[:], [[1, 128]], 0, 0, allow_small_or_imprecise_dtypes=True)], (), ("iom",))
+    V(64, lambda: [vc(T.ob[:, 15:143], T.ob0[:])], ("ob0",), ("ob",))
+    V(72, lambda: [vs(T.ob2[:], T.ob[:], 2.0, None, A.mult)], ("ob",), ("ob2",))
+    V(72, lambda: [vs(T.obn[:], T.ob[:], -1.0, None, A.mult)], ("ob",), ("obn",))
+    V(16 * 130, lambda: [vc(T.dg16[:, 129 * q:128 * q + 128:16], T.idb[:, q:128:16]) for q in range(16)], ("idb",), ("dg16",))
+    for nm, v in (("i592", 592.0), ("i16", 16.0), ("ni16", -16.0), ("ni32", -1.0)):
+        V(128, lambda nm=nm, v=v: [vs(T[nm][:], T.i32[:], v, None, A.mult)], ("i32",), (nm,))
+    V(64, lambda: [vs(T.pm[:], T.pi[:], 15, None, A.bitwise_and)], ("pi",), ("pm",))
+    V(64, lambda: [vc(T.pmf[:], T.pm[:])], ("pm",), ("pmf",))
+    V(64, lambda: [vc(T.pf[:], T.pi[:])], ("pi",), ("pf",))
+    V(64, lambda: [vt(T.bse[:], T.pf[:], T.pmf[:], A.subtract)], ("pf", "pmf"), ("bse",))
+    V(64, lambda: [vs(T.vb[:], T.pmf[:], -1.0, 65536.0, A.mult, A.add)], ("pmf",), ("vb",))
+    V(64, lambda: [vc(T.thf[:], T.thi[:])], ("thi",), ("thf",))
+    V(64, lambda: [vs(T.thb[:], T.thi[:], -32768.0, 16384.0, A.mult, A.add)], ("thi",), ("thb",))
+    V(64, lambda: [vc(T.sgf[:], T.sgi[:])], ("sgi",), ("sgf",))
+    V(64, lambda: [vs(T.tif[:], T.tii[:], T.bse[:], None, A.add)], ("tii", "bse"), ("tif",))
+    for k in range(3):
+        V(128, lambda k=k: [vs(T.gk[:, 128 * k:128 * k + 128], T.iom[:], T.tif[:, k:k + 1], T.sgf[:, k:k + 1], A.is_equal, A.mult)],
+          ("iom", "tif", "sgf"), (("gk", k),))
+    V(256, lambda: [vt(T.gs1[:], T.gk[:, 0:128], T.gk[:, 128:256], A.add)], (("gk", 0), ("gk", 1)), ("gs1",))
+    V(256, lambda: [vt(T.gj[:], T.gs1[:], T.gk[:, 256:384], A.add)], ("gs1", ("gk", 2)), ("gj",))
+    S(128, lambda: [act(T.ga[:], T.gj[:], F.Abs, scale=16384.0)], ("gj",), ("ga",))
+    V(64, lambda: [vs(T.nga[:], T.ga[:], -1.0, None, A.mult)], ("ga",), ("nga",))
+    q0 = tile()
+    P(128, lambda: [mm(pslice(q0, 0, 128), T.gj[:], T.idb[:], True, True)], ("gj", "idb"), (), (q0,))
+    S(128, lambda: [act(T.gt[:], pslice(q0, 0, 128), F.Copy)], (), ("gt",), (q0,))
+
+    for t in range(R):
+        a, b = 256 * t, 256 * t + 256
+        dst = T.cores[(me + 1 + t) % 4]
+        V(256, lambda t=t, a=a, b=b: [vc(T.le[:, a:b], T.dt[:, t:4096:16])], ("D",), (("le", t),))
+        V(256, lambda t=t, a=a, b=b: [vs(T.eb[:, a:b], T.dt[:, t:4096:16], 12288.0, None, A.add)], ("D",), (("eb", t),))
+        S(256, lambda t=t, a=a, b=b: [act(T.xn[:, a:b], T.xt[:, t:4096:16], F.Copy, scale=-1.0)], ("X",), (("xn", t),))
+        send(dst, (("xn", t),), T.xc[:, a:b], T.xn[:, a:b], "ax%d" % t, (("xc", t),))
+        send(dst, (("eb", t),), T.ec[:, a:b], T.eb[:, a:b], "ae%d" % t, (("ec", t),))
+
+    def dgather(c, lst, lo, out, rd, wr):
+        o, n = CH[c]
+        V(16 * n * GA, lambda: [vs(out[:, 16 * o:16 * o + 16 * n], T.dt[:, 0:4096].indirect(lst[:, lo + o:lo + o + n]), -2048.0, None, A.add)],
+          ("D",) + rd, wr)
+
+    def diag(c, src, q, a, rd):
+        o, n = CH[c]
+        P(16 * max(n, 64), lambda: [mm(pslice(q, a, n), T.dg16[:, 128 * p:128 * p + 128], src[:, 16 * o + p:16 * o + 16 * n:16], p == 0, p == 15)
+                                    for p in range(16)], rd + ("dg16",), (), (q,))
+
+    def viewdiff(c, eng, name, lst, lo, xneg, xo, yb, bb, rd, xkey, par, wide=4096):
+        o, n = CH[c]
+        w = 16 * n
+        if eng == "S":
+            S(w * GA, lambda: [act(yb[:, 16 * o:16 * o + w], T.xt[:, 0:wide].indirect(lst[:, lo + o:lo + o + n]), F.Copy)], ("X",) + rd, ((name, "y", c),))
+            pp = max(x for x in (1, 2, 4, 8, 16) if x * n <= 512)
+            for h in range(16 // pp):
+                q = tile()
+
+                def pf(h=h, q=q):
+                    r = []
+                    for k in range(pp):
+                        p = h * pp + k
+                        r.append(mm(pslice(q, n * k, n), T.idb[:], yb[:, 16 * o + p:16 * o + w:16], True, False))
+                        r.append(mm(pslice(q, n * k, n), T.idb[:], xneg[:, xo + o:xo + o + n], False, True))
+                    return r
+                P(2 * pp * max(n, 64), pf, ((name, "y", c), "idb", xkey), (), (q,))
+                S(pp * n, lambda h=h, q=q: [act(bb[:, 16 * o + h * pp * n:16 * o + (h + 1) * pp * n], pslice(q, 0, pp * n), F.Abs)], (), ((name, "b", c, h),), (q,))
+            return (lambda p: bb[:, 16 * o + p * n:16 * o + (p + 1) * n], None), tuple((name, "b", c, h) for h in range(16 // pp))
+        V(w * GA, lambda: [vt(yb[:, 16 * o:16 * o + w], T.xt[:, 0:wide].indirect(lst[:, lo + o:lo + o + n]), T.xr[:, 4096 * par + 16 * o:4096 * par + 16 * o + w], A.add)],
+          ("X",) + tuple(("xr", par, p) for p in range(16)) + rd, ((name, "y", c),))
+        if eng == "R":
+            V(w // 2, lambda: [vs(bb[:, 16 * o:16 * o + w], yb[:, 16 * o:16 * o + w], 0.0, None, A.max)], ((name, "y", c),), ((name, "b", c, 0),))
+            return (lambda p: bb[:, 16 * o + p:16 * o + w:16], yb), ((name, "b", c, 0), (name, "y", c))
+        S(w, lambda: [act(bb[:, 16 * o:16 * o + w], yb[:, 16 * o:16 * o + w], F.Abs)], ((name, "y", c),), ((name, "b", c, 0),))
+        return (lambda p: bb[:, 16 * o + p:16 * o + w:16], None), ((name, "b", c, 0),)
+
+    def dist(c, q, slices, rd, extra=None, xrd=()):
+        o, n = CH[c]
+        sl, rl = slices
+
+        def pf():
+            ob = T.ob if rl is None else T.ob2
+            r = [mm(pslice(q, 0, n), ob[:, 15 - p:143 - p], sl(p), p == 0, p == 15 and extra is None and rl is None) for p in range(16)]
+            if rl is not None:
+                r += [mm(pslice(q, 0, n), T.obn[:, 15 - p:143 - p], rl[:, 16 * o + p:16 * o + 16 * n:16], False, p == 15 and extra is None) for p in range(16)]
+            if extra is not None:
+                r.append(mm(pslice(q, 0, n), T.idb[:], extra(), False, True))
+            return r
+        P((17 if rl is None else 33) * max(n, 64), pf, rd + ("ob", "ob2", "obn", "idb") + xrd, (), (q,))
+
+    def rests(k, c, q, out, wr):
+        n = CH[c][1]
+        if RK[k - 1] == "V":
+            V(n, lambda: [vs(out(), pslice(q, 0, n), T.thf[:], 16384.0, A.is_ge, A.mult)], ("thf",), wr, (q,))
+        else:
+            S(n, lambda: [act(out(), pslice(q, 0, n), F.Relu, scale=32768.0, bias=T.thb[:])], ("thb",), wr, (q,))
+
+    wg, rg = {}, {}
+    for sizes, d in ((WG, wg), (RG, rg)):
+        a = 0
+        for x in sizes:
+            d[a + x - 1] = a
+            a += x
+    for t in range(R):
+        s = T.cores[(me + 1 + t) % 4]
+        home = T.cores[(me - 1 - t) % 4]
+        par = t % 2
+        a3, qb = 256 * t, 520 * t
+        for p in range(16):
+            gq(256, lambda p=p, par=par, a3=a3: [g.affine_select(T.xr[:, 4096 * par + p:4096 * par + 4096:16], T.xc[:, a3:a3 + 256], [[0, 256]], A.is_gt, 0.0, 1, 0)],
+               (("xc", t),), (("xr", par, p),))
+        gq(256, lambda a3=a3: [g.affine_select(T.nk[:, 0:1024:4], T.ec[:, a3:a3 + 256], [[0, 256]], A.is_gt, 0.0, 1, 0)], (("ec", t),), [("nk", c, 0) for c in range(NC)])
+        for c in range(NC):
+            o, n = chunk(c)
+            dgather(c, T.le, a3, T.g0, (("le", t),), (("g0", c),))
+            q = tile()
+            diag(c, T.g0, q, 0, (("g0", c),))
+            V(n, lambda q=q, o=o, n=n, a3=a3: [vs(T.l1[:, a3 + o:a3 + o + n], pslice(q, 0, n), 2048.0, None, A.add)], (), (("l1", t, c),), (q,))
+            send(s, (("l1", t, c),), T.ll1[:, a3 + o:a3 + o + n], T.l1[:, a3 + o:a3 + o + n], "al%d_%d" % (t, c), (("ll1", t, c),))
+        for c in range(NC):
+            o, n = chunk(c)
+            sl, rd = viewdiff(c, "S", "v1", T.l1, a3, T.xn, a3, T.y1, T.b1, (("l1", t, c),), ("xn", t), par)
+            q = tile()
+            dist(c, q, sl, rd)
+            rests(1, c, q, lambda o=o, n=n, a3=a3: T.r1[:, a3 + o:a3 + o + n], (("r1", t, c),))
+            if c in rg:
+                f = rg[c]
+                a, b = a3 + CH[f][0], a3 + o + n
+                send(s, [("r1", t, x) for x in range(f, c + 1)], T.lr1[:, a:b], T.r1[:, a:b], "ar%d_%d" % (t, c), [("lr1", t, x) for x in range(f, c + 1)])
+        for c in range(NC):
+            o, n = chunk(c)
+            for k, lst, lo, lk, gb, lout in ((2, T.ll1, a3, ("ll1", t, c), T.g1, T.l2), (3, T.l2, 0, ("l2", c), T.g2, T.l3)):
+                dgather(c, lst, lo, gb, (lk,), (("g", k, c),))
+                q = tile()
+                diag(c, gb, q, 0, (("g", k, c),))
+                V(n, lambda q=q, o=o, n=n, lout=lout: [vs(lout[:, o:o + n], pslice(q, 0, n), 2048.0, None, A.add)], (), (("l%d" % k, c),), (q,))
+                S(n, lambda q=q, o=o, n=n, k=k: [act(T.nk[:, 4 * o + k:4 * o + 4 * n:4], pslice(q, 0, n), F.Copy, bias=2048.0 + 4096.0 * (3 - k))], (), (("nk", c, k),), (q,))
+            V(n, lambda o=o, n=n, a3=a3: [vs(T.nk[:, 4 * o + 1:4 * o + 4 * n:4], T.ll1[:, a3 + o:a3 + o + n], 8192.0, None, A.add)], (("ll1", t, c),), (("nk", c, 1),))
+            S(n, lambda o=o, n=n, a3=a3: [act(T.r4[:, 4 * o + 1:4 * o + 4 * n:4], T.lr1[:, a3 + o:a3 + o + n], F.Copy)], (("lr1", t, c),), (("r4", c, 1),))
+        for c in range(NC):
+            o, n = chunk(c)
+            sl, rd = viewdiff(c, ENG2[c], "v2", T.l2, 0, T.xc, a3, T.y2, T.b2, (("l2", c),), ("xc", t), par)
+            q = tile()
+            dist(c, q, sl, rd, lambda o=o, n=n, a3=a3: T.lr1[:, a3 + o:a3 + o + n], (("lr1", t, c),))
+            rests(2, c, q, lambda o=o, n=n: T.r4[:, 4 * o + 2:4 * o + 4 * n:4], (("r4", c, 2),))
+        for c in range(NC):
+            o, n = chunk(c)
+            sl, rd = viewdiff(c, ENG3[c], "v3", T.l3, 0, T.xc, a3, T.y3, T.b3, (("l3", c),), ("xc", t), par)
+            q = tile()
+            dist(c, q, sl, rd, lambda o=o, n=n: T.r4[:, 4 * o + 2:4 * o + 4 * n:4], (("r4", c, 2),))
+            rests(3, c, q, lambda o=o, n=n: T.r4[:, 4 * o + 3:4 * o + 4 * n:4], (("r4", c, 3),))
+            V(4 * n, lambda o=o, n=n: [scan(T.es[:, 4 * o:4 * o + 4 * n], T.r4[:, 4 * o:4 * o + 4 * n], T.nk[:, 4 * o:4 * o + 4 * n], 0.0, A.min, A.max)],
+              [("r4", c, k) for k in range(4)] + [("nk", c, k) for k in range(4)], (("es", c),))
+            V(n, lambda o=o, n=n: [vc(T.l4[:, o:o + n], T.es[:, 4 * o + 3:4 * o + 4 * n:4])], (("es", c),), (("l4", c),))
+        if t == R - 1:
+            V(256, lambda: [vc(T.ei[:], T.es[:, 3:1024:4])], [("es", c) for c in range(NC)], ("ei",))
+            V(256, lambda: [vs(T.ef[:], T.ei[:], 4095, None, A.bitwise_and)], ("ei",), ("ef",))
+            V(256, lambda: [vc(T.yef[:], T.ef[:])], ("ef",), ("yef",))
+            send(home, ("yef",), T.yel[:], T.yef[:], "aye", ("yel",))
+        for c in range(NC):
+            o, n = chunk(c)
+            sl, rd = viewdiff(c, ENG4[c], "v4", T.l4, 0, T.xc, a3, T.y4, T.b4, (("l4", c), ("X4", 1), ("X4", 2), ("X4", 3)), ("xc", t), par, 16384)
+            q = tile()
+            diag(c, T.y4, q, 0, (("v4", "y", c),))
+            if ENG4[c] == "S":
+                tasks[-1]["dur"] += 64 * PC
+                f0 = tasks[-1]["fn"]
+
+                def pf(q=q, o=o, n=n, a3=a3):
+                    r = [mm(pslice(q, 0, n), T.dg16[:, 128 * p:128 * p + 128], T.y4[:, 16 * o + p:16 * o + 16 * n:16], p == 0, False) for p in range(16)]
+                    return r + [mm(pslice(q, 0, n), T.idb[:], T.xc[:, a3 + o:a3 + o + n], False, True)]
+                tasks[-1]["fn"] = pf
+            S(n, lambda q=q, o=o, n=n: [act(T.bb[:, o:o + n], pslice(q, 0, n), F.Sign, bias=-0.5)], (), (("bb", c),), (q,))
+            q = tile()
+            dist(c, q, sl, rd)
+            S(n, lambda q=q, o=o, n=n: [act(T.val[:, o:o + n], pslice(q, 0, n), F.Identity, scale=-16.0, bias=T.vb[:])], ("vb",), (("val", c),), (q,))
+            q = tile()
+            P(64, lambda q=q, o=o, n=n: [mm(pslice(q, 0, n), T.gt[:], T.bb[:, o:o + n], True, True)], ("gt", ("bb", c)), (), (q,))
+            S(n, lambda q=q, o=o, n=n: [act(T.sq[:, o:o + n], pslice(q, 0, n), F.Square)], (), (("sq", c),), (q,))
+            q = tile()
+            P(128, lambda q=q, o=o, n=n: [mm(pslice(q, 0, n), T.ga[:], T.sq[:, o:o + n], True, False),
+                                          mm(pslice(q, 0, n), T.nga[:], T.one[:, 0:n], False, True)], ("ga", "nga", "one", ("sq", c)), (), (q,))
+            V(n, lambda q=q, o=o, n=n: [vt(T.key[:, o:o + n], pslice(q, 0, n), T.val[:, o:o + n], A.min)], (("val", c),), (("key", c),), (q,))
+            q = tile()
+            P(512, lambda q=q, o=o, n=n: [mm(pslice(q, 0, 128, n), T.key[:, o:o + n], T.i32[:], True, True)], (("key", c), "i32"), (), (q,))
+            V(128, lambda q=q, c=c, n=n: [scan(T.ks[0:n, 128 * c:128 * c + 128], T.rs[0:n, :], pslice(q, 0, 128, n), 0.0, A.mult, A.max)],
+              ("rs",), (("ks", c),), (q,))
+            q = tile()
+            P(4 * 64, lambda q=q, c=c, n=n: [mm(pslice(q, 0, n, 8), T.ks[0:n, 128 * c + 15:128 * c + 128:16], T.i32[0:n, 0:n], True, True)], (("ks", c), "i32"), (), (q,))
+            S(n, lambda q=q, o=o, n=n: [act(T.mx[:, o:o + n], pslice(q, 0, n, 8), F.Copy)], (), (("mx", c),), (q,))
+            S(n + 150, lambda q=q, c=c, o=o, n=n: [act(T.cm[:, o:o + n], pslice(q, 0, n, 8), F.Sign, accum_out=T.cn[:, c:c + 1])], (), (("cn", c),), (q,))
+            q = tile()
+            P(4 * 64, lambda q=q, o=o, n=n: [mm(pslice(q, 0, n), T.ex[:], T.mx[:, o:o + n], True, True)], ("ex", ("mx", c)), (), (q,))
+            V(n, lambda q=q, o=o, n=n: [vt(T.lt[:, o:o + n], pslice(q, 0, n), T.key[:, o:o + n], A.is_gt)], (("key", c),), (("lt", c),), (q,))
+            V(2 * n, lambda o=o, n=n, qb=qb: [vt(T.qg[:, qb + 2 * o + 1:qb + 2 * o + 2 * n:2], T.lt[:, o:o + n], T.key[:, o:o + n], A.min)], (("key", c), ("lt", c)), (("go", t, c),))
+            q = tile()
+            P(12 * n, lambda q=q, o=o, n=n, a3=a3: [mm(pslice(q, 0, n), T.i592[:], T.es[:, 4 * o + 3:4 * o + 4 * n:4], True, False),
+                                                    mm(pslice(q, 0, n), T.ni16[:], T.ec[:, a3 + o:a3 + o + n], False, False),
+                                                    mm(pslice(q, 0, n), T.ni32[:], T.val[:, o:o + n], False, True)],
+              ("i592", "ni16", "ni32", ("es", c), ("ec", t), ("val", c)), (), (q,))
+            V(n, lambda q=q, o=o, n=n, qb=qb: [vt(T.gu[:, o:o + n], pslice(q, 0, n), T.qg[:, qb + 2 * o + 1:qb + 2 * o + 2 * n:2], A.mult)],
+              (("go", t, c),), (("gu", c),), (q,))
+            q = tile()
+            P(8 * n, lambda q=q, o=o, n=n, a3=a3: [mm(pslice(q, 0, n), T.i32[:], T.gu[:, o:o + n], True, False),
+                                                   mm(pslice(q, 0, n), T.i16[:], T.ec[:, a3 + o:a3 + o + n], False, True)],
+              ("i32", "i16", ("gu", c), ("ec", t)), (), (q,))
+            S(n, lambda q=q, o=o, n=n, qb=qb: [act(T.qg[:, qb + 2 * o:qb + 2 * o + 2 * n:2], pslice(q, 0, n), F.Copy)], (), (("qs", t, c),), (q,))
+            if c == NC - 1:
+                q = tile()
+                P(256, lambda q=q: [mm(pslice(q, 0, NC), T.o16[:], T.cn[:], True, True)], ["o16"] + [("cn", x) for x in range(NC)], (), (q,))
+                V(64, lambda q=q, qb=qb: [g.vector.tensor_reduce(T.qg[:, qb + 512:qb + 513], pslice(q, 0, NC), AxisListType.X, A.add)], (), (("a16", t),), (q,))
+            if c in wg:
+                f = wg[c]
+                a, b = qb + 2 * CH[f][0], qb + 2 * o + 2 * n + (c == NC - 1)
+                send(home, [(k, t, x) for x in range(f, c + 1) for k in ("qs", "go")] + ([("a16", t)] if c == NC - 1 else []),
+                     T.ql[:, a:b], T.qg[:, a:b], "aw%d_%d" % (t, c), [("wl", t, x) for x in range(f, c + 1)])
+        cur[0] = 0.0
+        V(256, lambda qb=qb: [vs(T.gaa[:], T.ql[:, qb + 1:qb + 512:2], T.ql[:, qb + 512:qb + 513], None, A.mult)], [("wl", t, c) for c in range(NC)], ("gaa",))
+        V(512, lambda qb=qb: [vt(T.wf[:], T.ql[:, qb:qb + 512:2], T.gaa[:], A.add)], ["gaa"], ("wf",))
+        if t < R - 1:
+            V(256, lambda t=t, a3=a3: [vs(T.dt[:, t:4096:16], T.wf[:], 4, 4095, A.arith_shift_right, A.bitwise_and)], ("wf",), ("D",))
+            V(256, lambda t=t, a3=a3: [vc(T.ydf[:, a3:a3 + 256], T.dt[:, t:4096:16])], ("D",), (("ydf", t),))
+        else:
+            V(256, lambda: [vs(T.ei[:], T.wf[:], 4, 4095, A.arith_shift_right, A.bitwise_and)], ("wf",), ("ei",))
+            V(256, lambda a3=a3: [vc(T.ydf[:, a3:a3 + 256], T.ei[:])], ("ei",), (("ydf", t),))
+        load("Y", lambda a3=a3: g.sync.dma_start(T.yd[:, a3:a3 + 256], T.ydf[:, a3:a3 + 256]), 2.0, (("ydf", t),), (("yd", t),))
+    load("Y", lambda: g.sync.dma_start(T.ye[:], T.yel[:]), 2.0, ("yel",), ("ye",))
+
+    n = len(tasks)
+    succ = [[] for _ in range(n)]
+    for i in range(n):
+        for d in tasks[i]["deps"]:
+            succ[d].append(i)
+    rank = [0.0] * n
+    for i in range(n - 1, -1, -1):
+        rank[i] = tasks[i]["dur"] + tasks[i]["lag"] + max([rank[j] for j in succ[i]] + [0.0])
+    left = [len(tasks[i]["deps"]) for i in range(n)]
+    ready_at, end = [0.0] * n, [0.0] * n
+    ready = [i for i in range(n) if left[i] == 0]
+    free, owner, order, done = {}, [None] * 8, [], set()
+
+    def bank_time(b):
+        if owner[b] is None:
+            return 0.0
+        u = tiles[owner[b]]["users"]
+        if any(x not in done for x in u):
+            return None
+        return max(end[x] for x in u)
+    while ready:
+        best = None
+        bts = [(bank_time(b), b) for b in range(8)]
+        bts = [x for x in bts if x[0] is not None]
+        for i in ready:
+            tk = tasks[i]
+            st = max(ready_at[i], free.get(tk["eng"], 0.0) if tk["eng"] != "R" else 0.0)
+            nb = [q for q in tk["tl"] if tiles[q]["bank"] < 0]
+            if nb:
+                if not bts:
+                    continue
+                st = max(st, min(bts)[0])
+            k = (round(st, 4), -rank[i] - tk["bias"], i)
+            if best is None or k < best[0]:
+                best = (k, i, st, nb)
+        _, i, st, nb = best
+        tk = tasks[i]
+        for q in nb:
+            b = min(bts)[1]
+            if owner[b] is not None:
+                tk["deps"] |= set(tiles[owner[b]]["users"])
+            owner[b] = q
+            tiles[q]["bank"] = b
+        end[i] = st + tk["dur"] + tk["lag"]
+        free[tk["eng"]] = st + tk["dur"]
+        done.add(i)
+        ready.remove(i)
+        order.append(i)
+        for j in succ[i]:
+            left[j] -= 1
+            ready_at[j] = max(ready_at[j], end[i])
+            if left[j] == 0:
+                ready.append(j)
+    assert len(order) == n
+
+    queue = {"V": g.vector, "S": g.scalar, "P": g.tensor, "G": g, "DMAY": g.sync, "DMAS": g.scalar}
+    cnt = {"V": 0, "S": 0, "P": 0, "G": 0}
+    know = {q: {} for q in ("V", "S", "P", "G", "DMAY")}
+    fin = [None] * n
+    for i in order:
+        tk = tasks[i]
+        if tk["eng"] == "R":
+            fin[i] = (tk["wait"][0], tk["wait"][1], {tk["wait"][0]: tk["wait"][1]})
+            continue
+        kn = know["S" if tk["eng"] == "DMAS" else tk["eng"]]
+        need = {}
+        for d in tk["deps"]:
+            if fin[d] is not None and need.get(fin[d][0], (0,))[0] < fin[d][1]:
+                need[fin[d][0]] = fin[d][1:]
+        for sname in sorted(need, key=lambda x: (-len(need[x][1]), x)):
+            v, kk = need[sname]
+            if kn.get(sname, 0) < v:
+                queue[tk["eng"]].wait_ge(T.sem[sname], v)
+                for x in kk:
+                    if kn.get(x, 0) < kk[x]:
+                        kn[x] = kk[x]
+        calls = tk["fn"]()
+        if tk["eng"] in cnt:
+            sname = SEMOF[tk["eng"]]
+            for x in calls:
+                cnt[tk["eng"]] += 1
+                x.then_inc(T.sem[sname], 1)
+            if calls:
+                kk = dict(kn)
+                kk[sname] = cnt[tk["eng"]]
+                fin[i] = (sname, cnt[tk["eng"]], kk)
+        else:
+            calls.then_inc(T.sem[tk["sem"]], 16)
+    for e in cnt:
+        g.wait_ge(T.sem[SEMOF[e]], cnt[e])
+    g.wait_ge(T.sem.ls, sends[0])
+    for k in range(dmas[0]):
+        g.wait_ge(T.sem["d%d" % k], 16)

@@ -1,57 +1,60 @@
-from concourse.bass import DstId, RemoteDMATransfer
-from concourse.mybir import AluOpType as A, AxisListType, ActivationFunctionType as F
+from concourse.mybir import AluOpType as A, ActivationFunctionType as F
 
-SIZES = [64, 64, 64, 64]
+SIZES = [112, 88, 56]
 CH = [(sum(SIZES[:i]), n) for i, n in enumerate(SIZES)]
 NC = len(CH)
 R = 3
-ENG2, ENG3, ENG4 = "SSSV", "VVSS", "VVVV"
-WG, RG = [2, 1, 1], [2, 2]
-BIAS = [2.0]
-RK = ["V", "V", "V"]
+HM = [0, 1, 1]
+ENG2, ENG3, ENG4 = "SSS", "RVS", "VVV"
+LOW = [1, 0, 0]
+WG, RG = [1, 1, 1], [1, 2]
+BIAS = [0.5]
+RK = ["S", "S", "V"]
 SCRATCH = {
-    "dt": ("sbuf", [128, 4096], "int32"), "xt": ("sbuf", [128, 16384], "bfloat16"),
+    "dt": ("sbuf", [128, 4096], "int32"), "xt": ("sbuf", [128, 4096], "bfloat16"),
     "thi": ("sbuf", [128, 1], "int32"), "tii": ("sbuf", [128, 3], "int32"), "sgi": ("sbuf", [128, 3], "int32"),
-    "thf": ("sbuf", [128, 1], "float32"), "thb": ("sbuf", [128, 1], "float32"), "tif": ("sbuf", [128, 3], "float32"), "sgf": ("sbuf", [128, 3], "float32"),
+    "thf": ("sbuf", [128, 2], "float32"), "tif": ("sbuf", [128, 3], "float32"), "sgf": ("sbuf", [128, 3], "float32"),
     "pi": ("sbuf", [128, 1], "int32"), "pm": ("sbuf", [128, 1], "int32"), "pf": ("sbuf", [128, 1], "float32"),
     "pmf": ("sbuf", [128, 1], "float32"), "vb": ("sbuf", [128, 1], "float32"), "bse": ("sbuf", [128, 1], "float32"),
-    "one": ("sbuf", [128, 128], "bfloat16"), "ob0": ("sbuf", [128, 128], "bfloat16"), "ob": ("sbuf", [128, 144], "bfloat16"), "ob2": ("sbuf", [128, 144], "bfloat16"), "obn": ("sbuf", [128, 144], "bfloat16"),
+    "one": ("sbuf", [128, 128], "bfloat16"), "ob0": ("sbuf", [128, 128], "bfloat16"), "ob": ("sbuf", [128, 144], "bfloat16"),
+    "ob2": ("sbuf", [128, 144], "bfloat16"), "obn": ("sbuf", [128, 144], "bfloat16"),
     "one32": ("sbuf", [128, 128], "float32"), "idb": ("sbuf", [128, 128], "bfloat16"), "i32": ("sbuf", [128, 128], "float32"),
     "ni32": ("sbuf", [128, 128], "float32"), "i592": ("sbuf", [128, 128], "float32"), "i16": ("sbuf", [128, 128], "float32"),
     "ni16": ("sbuf", [128, 128], "float32"), "dg16": ("sbuf", [128, 2048], "bfloat16"), "ex": ("sbuf", [8, 128], "float32"),
     "rs": ("sbuf", [128, 128], "float32"), "o16": ("sbuf", [8, 128], "float32"),
     "iom": ("sbuf", [128, 128], "float32"), "gk": ("sbuf", [128, 384], "float32"), "gs1": ("sbuf", [128, 128], "float32"),
-    "gj": ("sbuf", [128, 128], "bfloat16"), "ga": ("sbuf", [128, 128], "bfloat16"), "nga": ("sbuf", [128, 128], "bfloat16"),
-    "gt": ("sbuf", [128, 128], "bfloat16"),
-    "le": ("sbuf", [128, 768], "uint16"), "eb": ("sbuf", [128, 768], "float32"), "xn": ("sbuf", [128, 768], "bfloat16"),
-    "xc": ("sbuf", [128, 768], "bfloat16"), "ec": ("sbuf", [128, 768], "float32"), "xr": ("sbuf", [128, 8192], "bfloat16"),
+    "gj": ("sbuf", [128, 128], "bfloat16"), "gm": ("sbuf", [128, 384], "bfloat16"), "gml": ("sbuf", [128, 1152], "bfloat16"),
+    "thl": ("sbuf", [128, 6], "float32"),
+    "le": ("sbuf", [128, 768], "uint16"), "eb": ("sbuf", [128, 768], "float32"), "eb16": ("sbuf", [128, 768], "float32"),
+    "xn": ("sbuf", [128, 768], "bfloat16"), "xc": ("sbuf", [128, 768], "bfloat16"), "ec": ("sbuf", [128, 768], "float32"),
+    "xo": ("sbuf", [128, 8192], "bfloat16"), "xs1": ("sbuf", [128, 4096], "bfloat16"), "xs2": ("sbuf", [128, 4096], "bfloat16"),
     "l1": ("sbuf", [128, 768], "uint16"), "ll1": ("sbuf", [128, 768], "uint16"),
+    "l2": ("sbuf", [128, 768], "uint16"), "ll2": ("sbuf", [128, 768], "uint16"),
+    "l3": ("sbuf", [128, 768], "uint16"), "ll3": ("sbuf", [128, 768], "uint16"), "l4": ("sbuf", [128, 256], "uint16"),
     "r1": ("sbuf", [128, 768], "bfloat16"), "lr1": ("sbuf", [128, 768], "bfloat16"),
-    "l2": ("sbuf", [128, 256], "uint16"), "l3": ("sbuf", [128, 256], "uint16"), "l4": ("sbuf", [128, 256], "uint16"),
-    "g0": ("sbuf", [128, 4096], "float16"), "g1": ("sbuf", [128, 4096], "float16"), "g2": ("sbuf", [128, 4096], "float16"),
-    "y1": ("sbuf", [128, 4096], "bfloat16"), "y2": ("sbuf", [128, 4096], "bfloat16"), "y3": ("sbuf", [128, 4096], "bfloat16"),
-    "y4": ("sbuf", [128, 4096], "bfloat16"),
-    "b1": ("sbuf", [128, 4096], "bfloat16"), "b2": ("sbuf", [128, 4096], "bfloat16"), "b3": ("sbuf", [128, 4096], "bfloat16"),
-    "b4": ("sbuf", [128, 4096], "bfloat16"),
+    "g0": ("sbuf", [128, 4096], "float16"), "g1": ("sbuf", [128, 4096], "float16"),
+    "y1": ("sbuf", [128, 4096], "bfloat16"), "y2": ("sbuf", [128, 4096], "bfloat16"),
+    "b1": ("sbuf", [128, 4096], "bfloat16"), "b2": ("sbuf", [128, 4096], "bfloat16"),
     "nk": ("sbuf", [128, 1024], "float32"), "r4": ("sbuf", [128, 1024], "bfloat16"), "es": ("sbuf", [128, 1024], "float32"),
     "ei": ("sbuf", [128, 256], "int32"), "ef": ("sbuf", [128, 256], "int32"), "val": ("sbuf", [128, 256], "float32"),
     "bb": ("sbuf", [128, 256], "bfloat16"), "sq": ("sbuf", [128, 256], "bfloat16"), "key": ("sbuf", [128, 256], "float32"),
     "ks": ("sbuf", [128, 128 * NC], "float32"), "mx": ("sbuf", [8, 256], "float32"), "lt": ("sbuf", [128, 256], "bfloat16"),
-    "cm": ("sbuf", [8, 256], "bfloat16"), "cn": ("sbuf", [8, NC], "float32"),
-    "gu": ("sbuf", [128, 256], "float32"), "gaa": ("sbuf", [128, 256], "float32"),
-    "qg": ("sbuf", [128, 1560], "float32"), "ql": ("sbuf", [128, 1560], "float32"),
-    "wf": ("sbuf", [128, 256], "int32"), "ydf": ("sbuf", [128, 768], "float32"), "yef": ("sbuf", [128, 256], "float32"),
-    "yel": ("sbuf", [128, 256], "float32"),
+    "cm": ("sbuf", [8, 256], "bfloat16"), "cn": ("sbuf", [8, 1], "float32"),
+    "gu": ("sbuf", [128, 256], "float32"), "go": ("sbuf", [128, 256], "float32"), "a16": ("sbuf", [128, 1], "float32"),
+    "gaa": ("sbuf", [128, 256], "float32"), "qg": ("sbuf", [128, 520], "float32"), "ql": ("sbuf", [128, 520], "float32"),
+    "wf": ("sbuf", [128, 256], "int32"), "wi": ("sbuf", [128, 256], "int32"), "ydf": ("sbuf", [128, 768], "float32"), "yef": ("sbuf", [128, 256], "float32"),
 }
-for _i in range(8):
+for _i in range(4):
     SCRATCH["ps%d" % _i] = ("psum", [128, 512], "float32")
-SEMAPHORES = ["cv", "cs", "cp", "cg", "ls", "aye"]
-SEMAPHORES += ["d%d" % i for i in range(14)]
+for _i in range(2):
+    SCRATCH["ps%d" % (4 + _i)] = ("psum", [128, 1024], "float32")
+SEMAPHORES = ["cv", "cs", "cp", "cg", "ls"]
+SEMAPHORES += ["d%d" % i for i in range(20)]
 for _t in range(R):
-    SEMAPHORES += ["ax%d" % _t, "ae%d" % _t] + ["aw%d_%d" % (_t, _c) for _c in range(NC)]
-    SEMAPHORES += ["al%d_%d" % (_t, _c) for _c in range(NC)] + ["ar%d_%d" % (_t, _c) for _c in range(NC)]
+    SEMAPHORES += [x % _t for x in ("ax%d", "ae%d", "ag%d", "at%d")]
+    SEMAPHORES += [x % (_t, _c) for x in ("al%d_%d", "ar%d_%d", "aw%d_%d", "am%d_%d", "an%d_%d") for _c in range(NC)]
 SEMOF = {"V": "cv", "S": "cs", "P": "cp", "G": "cg"}
-CY, GA, VF, SF, PC, HOP, CALL = 0.00095, 1.5, 0.06, 0.07, 0.00048, 2.2, 0.8
+CY, GA, VF, SF, PC, HOP, CALL = 0.0009, 1.5, 0.13, 0.2, 0.00045, 2.8, 1.0
 
 
 def rank_program(g, core, T, topo):
@@ -94,8 +97,8 @@ def rank_program(g, core, T, topo):
         cur[0] = BIAS[0] * (NC - 1 - c)
         return CH[c]
 
-    def tile():
-        tiles.append({"users": [], "bank": -1})
+    def tile(wide=False):
+        tiles.append({"users": [], "bank": -1, "pool": (4, 5) if wide else (0, 1, 2, 3)})
         return len(tiles) - 1
 
     def pslice(q, a, n, P=128):
@@ -116,13 +119,17 @@ def rank_program(g, core, T, topo):
     def load(eng, fn, dur, rd=(), wr=()):
         k = dmas[0]
         dmas[0] += 1
-        i = add("DMA" + eng, 0.1, fn, rd, (), ())
+        i = add("DMA" + eng, 0.1, fn, rd, wr, ())
         tasks[i]["sem"] = "d%d" % k
         j = add("R", 0.0, None, (), wr, (), after=(i,), lag=dur)
         tasks[j]["wait"] = ("d%d" % k, 16)
 
-    def send(dst, src_key, out, in_, rsem, land_key):
-        es = topo.engines(core, dst)[0:8]
+    def send(dst, src_key, out, in_, rsem, land_key, big=False, low=False):
+        def pick(a, b):
+            e = topo.engines(a, b)
+            return e[len(e) // 2:] if big else e[:4] if low else e[:8]
+        es = pick(core, dst)
+        src = T.cores[(2 * me - T.rank_of(dst)) % 4]
         rid, pid, _ = topo.addr(dst)
         sends[0] += len(es)
 
@@ -130,21 +137,21 @@ def rank_program(g, core, T, topo):
             g.remote_dma(out, in_, T.sem[rsem], T.sem.ls, pid, rid, sum(1 << e for e in es))
             return []
         i = add("G", CALL, fn, src_key, (), ())
-        j = add("R", 0.0, None, (), land_key, (), after=(i,), lag=HOP)
-        tasks[j]["wait"] = (rsem, len(es))
+        j = add("R", 0.0, None, (), land_key, (), after=(i,), lag=14.0 if big else HOP)
+        tasks[j]["wait"] = (rsem, len(pick(src, core)))
 
     mm = g.tensor.matmul
     vc, vt, vs = g.vector.tensor_copy, g.vector.tensor_tensor, g.vector.tensor_scalar
     scan = g.vector.tensor_tensor_scan
     act = g.scalar.activation
 
-    load("Y", lambda: g.sync.dma_start(T.dt[:], T.dg[:]), 9.0, (), ("D",))
-    load("Y", lambda: g.sync.dma_start(T.xt[:, 0:4096], T.xv[:]), 12.0, (), ("X",))
-    load("S", lambda: g.scalar.dma_start(T.tii[:], T.ti[:]), 2.0, (), ("tii",))
-    load("S", lambda: g.scalar.dma_start(T.sgi[:], T.sg[:]), 2.0, (), ("sgi",))
-    load("S", lambda: g.scalar.dma_start(T.thi[:], T.th[:]), 2.0, (), ("thi",))
-    for k in range(1, 4):
-        load("Y", lambda k=k: g.sync.dma_start(T.xt[:, 4096 * k:4096 * k + 4096], T.xt[:, 0:4096]), 4.0, ("X",), (("X4", k),))
+    cur[0] = 1000.0
+    load("Y", lambda: g.sync.dma_start(T.tii[:], T.ti[:]), 3.0, (), ("tii",))
+    load("Y", lambda: g.sync.dma_start(T.sgi[:], T.sg[:]), 3.0, (), ("sgi",))
+    load("Y", lambda: g.sync.dma_start(T.thi[:], T.th[:]), 3.0, (), ("thi",))
+    cur[0] = 0.0
+    load("Y", lambda: g.sync.dma_start(T.dt[:], T.dg[:]), 8.0, (), ("D",))
+    load("Y", lambda: g.sync.dma_start(T.xt[:], T.xv[:]), 10.5, (), ("X",))
 
     V(64, lambda: [g.vector.memset(T.one[:], 1.0)], (), ("one",))
     V(128, lambda: [g.vector.memset(T.one32[:], 1.0)], (), ("one32",))
@@ -173,8 +180,8 @@ def rank_program(g, core, T, topo):
     V(64, lambda: [vc(T.pf[:], T.pi[:])], ("pi",), ("pf",))
     V(64, lambda: [vt(T.bse[:], T.pf[:], T.pmf[:], A.subtract)], ("pf", "pmf"), ("bse",))
     V(64, lambda: [vs(T.vb[:], T.pmf[:], -1.0, 65536.0, A.mult, A.add)], ("pmf",), ("vb",))
-    V(64, lambda: [vc(T.thf[:], T.thi[:])], ("thi",), ("thf",))
-    V(64, lambda: [vs(T.thb[:], T.thi[:], -32768.0, 16384.0, A.mult, A.add)], ("thi",), ("thb",))
+    V(64, lambda: [vc(T.thf[:, 0:1], T.thi[:])], ("thi",), ("thf",))
+    V(64, lambda: [vs(T.thf[:, 1:2], T.thi[:], -32768.0, 16384.0, A.mult, A.add)], ("thi",), ("thb",))
     V(64, lambda: [vc(T.sgf[:], T.sgi[:])], ("sgi",), ("sgf",))
     V(64, lambda: [vs(T.tif[:], T.tii[:], T.bse[:], None, A.add)], ("tii", "bse"), ("tif",))
     for k in range(3):
@@ -182,11 +189,11 @@ def rank_program(g, core, T, topo):
           ("iom", "tif", "sgf"), (("gk", k),))
     V(256, lambda: [vt(T.gs1[:], T.gk[:, 0:128], T.gk[:, 128:256], A.add)], (("gk", 0), ("gk", 1)), ("gs1",))
     V(256, lambda: [vt(T.gj[:], T.gs1[:], T.gk[:, 256:384], A.add)], ("gs1", ("gk", 2)), ("gj",))
-    S(128, lambda: [act(T.ga[:], T.gj[:], F.Abs, scale=16384.0)], ("gj",), ("ga",))
-    V(64, lambda: [vs(T.nga[:], T.ga[:], -1.0, None, A.mult)], ("ga",), ("nga",))
+    S(128, lambda: [act(T.gm[:, 128:256], T.gj[:], F.Abs, scale=16384.0)], ("gj",), ("ga",))
+    V(64, lambda: [vs(T.gm[:, 256:384], T.gm[:, 128:256], -1.0, None, A.mult)], ("ga",), ("nga",))
     q0 = tile()
     P(128, lambda: [mm(pslice(q0, 0, 128), T.gj[:], T.idb[:], True, True)], ("gj", "idb"), (), (q0,))
-    S(128, lambda: [act(T.gt[:], pslice(q0, 0, 128), F.Copy)], (), ("gt",), (q0,))
+    S(128, lambda: [act(T.gm[:, 0:128], pslice(q0, 0, 128), F.Copy)], (), ("gt",), (q0,))
 
     for t in range(R):
         a, b = 256 * t, 256 * t + 256
@@ -194,8 +201,14 @@ def rank_program(g, core, T, topo):
         V(256, lambda t=t, a=a, b=b: [vc(T.le[:, a:b], T.dt[:, t:4096:16])], ("D",), (("le", t),))
         V(256, lambda t=t, a=a, b=b: [vs(T.eb[:, a:b], T.dt[:, t:4096:16], 12288.0, None, A.add)], ("D",), (("eb", t),))
         S(256, lambda t=t, a=a, b=b: [act(T.xn[:, a:b], T.xt[:, t:4096:16], F.Copy, scale=-1.0)], ("X",), (("xn", t),))
-        send(dst, (("xn", t),), T.xc[:, a:b], T.xn[:, a:b], "ax%d" % t, (("xc", t),))
-        send(dst, (("eb", t),), T.ec[:, a:b], T.eb[:, a:b], "ae%d" % t, (("ec", t),))
+        if not HM[t]:
+            V(256, lambda a=a, b=b: [vs(T.eb16[:, a:b], T.eb[:, a:b], 16.0, None, A.mult)], (("eb", t),), (("eb16", t),))
+
+    def tables(t, rd):
+        dst = T.cores[(me - 1 - t) % 4]
+        send(dst, ("X",) + rd, T["xs%d" % t][:], T.xt[:], "ax%d" % t, (("XS", t),), big=True)
+        send(dst, ("ga", "nga", "gt") + rd, T.gml[:, 384 * t:384 * t + 384], T.gm[:], "ag%d" % t, (("gml", t),), low=True)
+        send(dst, ("thf", "thb") + rd, T.thl[:, 2 * t:2 * t + 2], T.thf[:], "at%d" % t, (("thl", t),), low=True)
 
     def dgather(c, lst, lo, out, rd, wr):
         o, n = CH[c]
@@ -207,14 +220,32 @@ def rank_program(g, core, T, topo):
         P(16 * max(n, 64), lambda: [mm(pslice(q, a, n), T.dg16[:, 128 * p:128 * p + 128], src[:, 16 * o + p:16 * o + 16 * n:16], p == 0, p == 15)
                                     for p in range(16)], rd + ("dg16",), (), (q,))
 
-    def viewdiff(c, eng, name, lst, lo, xneg, xo, yb, bb, rd, xkey, par, wide=4096):
+    def viewdiff(c, eng, name, tab, lst, lo, xneg, xo, yb, bb, rd, xkey, xrep, xbase):
         o, n = CH[c]
         w = 16 * n
         if eng == "S":
-            S(w * GA, lambda: [act(yb[:, 16 * o:16 * o + w], T.xt[:, 0:wide].indirect(lst[:, lo + o:lo + o + n]), F.Copy)], ("X",) + rd, ((name, "y", c),))
+            S(w * GA, lambda: [act(yb[:, 16 * o:16 * o + w], tab[0][:, 0:4096].indirect(lst[:, lo + o:lo + o + n]), F.Copy)], tab[1] + rd, ((name, "y", c),))
+            if xrep is not None:
+                keys = []
+                for a in range(0, w, 1024):
+                    m = min(1024, w - a)
+                    q = tile(True)
+
+                    def pf(a=a, m=m, q=q):
+                        r = []
+                        for e in range(0, m, 512):
+                            k = min(512, m - e)
+                            i = 16 * o + a + e
+                            r.append(mm(pslice(q, e, k), T.idb[:], yb[:, i:i + k], True, False))
+                            r.append(mm(pslice(q, e, k), T.idb[:], xrep[:, xbase + i:xbase + i + k], False, True))
+                        return r
+                    P(2 * m, pf, ((name, "y", c), "idb") + xkey, (), (q,))
+                    S(m, lambda a=a, m=m, q=q: [act(bb[:, 16 * o + a:16 * o + a + m], pslice(q, 0, m), F.Abs)], (), ((name, "b", c, a),), (q,))
+                    keys.append((name, "b", c, a))
+                return (lambda p: bb[:, 16 * o + p:16 * o + w:16], None), tuple(keys)
             pp = max(x for x in (1, 2, 4, 8, 16) if x * n <= 512)
             for h in range(16 // pp):
-                q = tile()
+                q = tile(True)
 
                 def pf(h=h, q=q):
                     r = []
@@ -223,18 +254,18 @@ def rank_program(g, core, T, topo):
                         r.append(mm(pslice(q, n * k, n), T.idb[:], yb[:, 16 * o + p:16 * o + w:16], True, False))
                         r.append(mm(pslice(q, n * k, n), T.idb[:], xneg[:, xo + o:xo + o + n], False, True))
                     return r
-                P(2 * pp * max(n, 64), pf, ((name, "y", c), "idb", xkey), (), (q,))
+                P(2 * pp * max(n, 64), pf, ((name, "y", c), "idb") + xkey, (), (q,))
                 S(pp * n, lambda h=h, q=q: [act(bb[:, 16 * o + h * pp * n:16 * o + (h + 1) * pp * n], pslice(q, 0, pp * n), F.Abs)], (), ((name, "b", c, h),), (q,))
             return (lambda p: bb[:, 16 * o + p * n:16 * o + (p + 1) * n], None), tuple((name, "b", c, h) for h in range(16 // pp))
-        V(w * GA, lambda: [vt(yb[:, 16 * o:16 * o + w], T.xt[:, 0:wide].indirect(lst[:, lo + o:lo + o + n]), T.xr[:, 4096 * par + 16 * o:4096 * par + 16 * o + w], A.add)],
-          ("X",) + tuple(("xr", par, p) for p in range(16)) + rd, ((name, "y", c),))
+        V(w * GA, lambda: [vt(yb[:, 16 * o:16 * o + w], tab[0][:, 0:4096].indirect(lst[:, lo + o:lo + o + n]), xrep[:, xbase + 16 * o:xbase + 16 * o + w], A.add)],
+          tab[1] + xkey + rd, ((name, "y", c),))
         if eng == "R":
             V(w // 2, lambda: [vs(bb[:, 16 * o:16 * o + w], yb[:, 16 * o:16 * o + w], 0.0, None, A.max)], ((name, "y", c),), ((name, "b", c, 0),))
             return (lambda p: bb[:, 16 * o + p:16 * o + w:16], yb), ((name, "b", c, 0), (name, "y", c))
         S(w, lambda: [act(bb[:, 16 * o:16 * o + w], yb[:, 16 * o:16 * o + w], F.Abs)], ((name, "y", c),), ((name, "b", c, 0),))
         return (lambda p: bb[:, 16 * o + p:16 * o + w:16], None), ((name, "b", c, 0),)
 
-    def dist(c, q, slices, rd, extra=None, xrd=()):
+    def dist(name, c, q, slices, rd, extra=None, xrd=()):
         o, n = CH[c]
         sl, rl = slices
 
@@ -246,14 +277,18 @@ def rank_program(g, core, T, topo):
             if extra is not None:
                 r.append(mm(pslice(q, 0, n), T.idb[:], extra(), False, True))
             return r
-        P((17 if rl is None else 33) * max(n, 64), pf, rd + ("ob", "ob2", "obn", "idb") + xrd, (), (q,))
+        P((17 if rl is None else 33) * max(n, 64), pf, rd + ("ob", "ob2", "obn", "idb", (name, "y", c)) + xrd, (), (q,))
 
-    def rests(k, c, q, out, wr):
+    def rests(k, c, q, out, wr, th, tk):
         n = CH[c][1]
         if RK[k - 1] == "V":
-            V(n, lambda: [vs(out(), pslice(q, 0, n), T.thf[:], 16384.0, A.is_ge, A.mult)], ("thf",), wr, (q,))
+            V(n, lambda: [vs(out(), pslice(q, 0, n), th[0][:, th[1]:th[1] + 1], 16384.0, A.is_ge, A.mult)], tk, wr, (q,))
         else:
-            S(n, lambda: [act(out(), pslice(q, 0, n), F.Relu, scale=32768.0, bias=T.thb[:])], ("thb",), wr, (q,))
+            S(n, lambda: [act(out(), pslice(q, 0, n), F.Relu, scale=32768.0, bias=th[0][:, th[1] + 1:th[1] + 2])], tk, wr, (q,))
+
+    def repeat(out, ob, src, sb, rd, u):
+        for p in range(16):
+            gq(256, lambda p=p: [g.affine_select(out[:, ob + p:ob + 4096:16], src[:, sb:sb + 256], [[0, 256]], A.is_gt, 0.0, 1, 0)], rd, (("xo", u, p),))
 
     wg, rg = {}, {}
     for sizes, d in ((WG, wg), (RG, rg)):
@@ -264,82 +299,116 @@ def rank_program(g, core, T, topo):
     for t in range(R):
         s = T.cores[(me + 1 + t) % 4]
         home = T.cores[(me - 1 - t) % 4]
-        par = t % 2
-        a3, qb = 256 * t, 520 * t
-        for p in range(16):
-            gq(256, lambda p=p, par=par, a3=a3: [g.affine_select(T.xr[:, 4096 * par + p:4096 * par + 4096:16], T.xc[:, a3:a3 + 256], [[0, 256]], A.is_gt, 0.0, 1, 0)],
-               (("xc", t),), (("xr", par, p),))
-        gq(256, lambda a3=a3: [g.affine_select(T.nk[:, 0:1024:4], T.ec[:, a3:a3 + 256], [[0, 256]], A.is_gt, 0.0, 1, 0)], (("ec", t),), [("nk", c, 0) for c in range(NC)])
+        hm, par = HM[t], t % 2
+        a3 = 256 * t
+        own = ("thf", "thb")
+        xown = tuple(("xo", par, p) for p in range(16))
+        if hm:
+            tab = (T["xs%d" % t], (("XS", t),))
+            xx, xbase, xkey = T.xn, 4096 * par, xown
+            ee, eek, th, tk = T.eb, ("eb", t), (T.thl, 2 * t), (("thl", t),)
+            gm, g0, gk, m1, m1k = T.gml, 384 * t, (("gml", t),), T.l1, "l1"
+            v2, v3, k2, k3 = T.ll2, T.ll3, "ll2", "ll3"
+        else:
+            tab = (T.xt, ("X",))
+            xx, xbase, xkey = T.xc, 0, tuple(("xo", 0, p) for p in range(16))
+            ee, eek, th, tk = T.ec, ("ec", t), (T.thf, 0), own
+            gm, g0, gk, m1, m1k = T.gm, 0, ("ga", "nga", "gt"), T.ll1, "ll1"
+            v2, v3, k2, k3 = T.l2, T.l3, "l2", "l3"
         for c in range(NC):
             o, n = chunk(c)
             dgather(c, T.le, a3, T.g0, (("le", t),), (("g0", c),))
             q = tile()
             diag(c, T.g0, q, 0, (("g0", c),))
             V(n, lambda q=q, o=o, n=n, a3=a3: [vs(T.l1[:, a3 + o:a3 + o + n], pslice(q, 0, n), 2048.0, None, A.add)], (), (("l1", t, c),), (q,))
-            send(s, (("l1", t, c),), T.ll1[:, a3 + o:a3 + o + n], T.l1[:, a3 + o:a3 + o + n], "al%d_%d" % (t, c), (("ll1", t, c),))
+            send(s, (("l1", t, c),), T.ll1[:, a3 + o:a3 + o + n], T.l1[:, a3 + o:a3 + o + n], "al%d_%d" % (t, c), (("ll1", t, c),), low=LOW[t])
+        cur[0] = 0.0
+        made = (("l1", t, NC - 1),)
+        if not hm:
+            send(s, (("xn", t),) + made, T.xc[:, a3:a3 + 256], T.xn[:, a3:a3 + 256], "ax%d" % t, (("xc", t),), low=LOW[t])
+            send(s, (("eb", t),) + made, T.ec[:, a3:a3 + 256], T.eb[:, a3:a3 + 256], "ae%d" % t, (("ec", t),), low=LOW[t])
+            repeat(T.xo, 0, T.xc, a3, (("xc", t),), 0)
+        if t == 0:
+            tables(1, made)
+        gq(256, lambda a3=a3, ee=ee: [g.affine_select(T.nk[:, 0:1024:4], ee[:, a3:a3 + 256], [[0, 256]], A.is_gt, 0.0, 1, 0)], (eek,) + made, [("nk", c, 0) for c in range(NC)])
+        if t < R - 1:
+            u = (t + 1) % 2
+            repeat(T.xo, 4096 * u, T.xn, a3 + 256, (("xn", t + 1),) + made, u)
         for c in range(NC):
             o, n = chunk(c)
-            sl, rd = viewdiff(c, "S", "v1", T.l1, a3, T.xn, a3, T.y1, T.b1, (("l1", t, c),), ("xn", t), par)
+            sl, rd = viewdiff(c, "S", "v1", (T.xt, ("X",)), T.l1, a3, T.xn, a3, T.y1, T.b1, (("l1", t, c),), xown if t else (("xn", t),), T.xo if t else None, 4096 * par)
             q = tile()
-            dist(c, q, sl, rd)
-            rests(1, c, q, lambda o=o, n=n, a3=a3: T.r1[:, a3 + o:a3 + o + n], (("r1", t, c),))
-            if c in rg:
+            dist("v1", c, q, sl, rd)
+            if hm:
+                rests(1, c, q, lambda o=o, n=n: T.r4[:, 4 * o + 1:4 * o + 4 * n:4], (("r4", c, 1),), (T.thf, 0), own)
+            else:
+                rests(1, c, q, lambda o=o, n=n, a3=a3: T.r1[:, a3 + o:a3 + o + n], (("r1", t, c),), (T.thf, 0), own)
+            if c in rg and not hm:
                 f = rg[c]
                 a, b = a3 + CH[f][0], a3 + o + n
-                send(s, [("r1", t, x) for x in range(f, c + 1)], T.lr1[:, a:b], T.r1[:, a:b], "ar%d_%d" % (t, c), [("lr1", t, x) for x in range(f, c + 1)])
+                send(s, [("r1", t, x) for x in range(f, c + 1)], T.lr1[:, a:b], T.r1[:, a:b], "ar%d_%d" % (t, c), [("lr1", t, x) for x in range(f, c + 1)], low=LOW[t])
+        if t == 0:
+            tables(2, (("lr1", 0, NC - 1),))
         for c in range(NC):
             o, n = chunk(c)
-            for k, lst, lo, lk, gb, lout in ((2, T.ll1, a3, ("ll1", t, c), T.g1, T.l2), (3, T.l2, 0, ("l2", c), T.g2, T.l3)):
-                dgather(c, lst, lo, gb, (lk,), (("g", k, c),))
+            for k, lst, lk, gb, gkey, lout in ((2, T.ll1, ("ll1", t, c), T.g1, ("g1", c), T.l2), (3, T.l2, ("l2", t, c), T.g0, ("g0", c), T.l3)):
+                dgather(c, lst, a3, gb, (lk,), (gkey,))
                 q = tile()
-                diag(c, gb, q, 0, (("g", k, c),))
-                V(n, lambda q=q, o=o, n=n, lout=lout: [vs(lout[:, o:o + n], pslice(q, 0, n), 2048.0, None, A.add)], (), (("l%d" % k, c),), (q,))
-                S(n, lambda q=q, o=o, n=n, k=k: [act(T.nk[:, 4 * o + k:4 * o + 4 * n:4], pslice(q, 0, n), F.Copy, bias=2048.0 + 4096.0 * (3 - k))], (), (("nk", c, k),), (q,))
-            V(n, lambda o=o, n=n, a3=a3: [vs(T.nk[:, 4 * o + 1:4 * o + 4 * n:4], T.ll1[:, a3 + o:a3 + o + n], 8192.0, None, A.add)], (("ll1", t, c),), (("nk", c, 1),))
-            S(n, lambda o=o, n=n, a3=a3: [act(T.r4[:, 4 * o + 1:4 * o + 4 * n:4], T.lr1[:, a3 + o:a3 + o + n], F.Copy)], (("lr1", t, c),), (("r4", c, 1),))
+                diag(c, gb, q, 0, (gkey,))
+                V(n, lambda q=q, o=o, n=n, lout=lout, a3=a3: [vs(lout[:, a3 + o:a3 + o + n], pslice(q, 0, n), 2048.0, None, A.add)], (), (("l%d" % k, t, c),), (q,))
+                if hm:
+                    land = (T.ll2, T.ll3)[k - 2]
+                    send(home, (("l%d" % k, t, c),), land[:, a3 + o:a3 + o + n], lout[:, a3 + o:a3 + o + n], ("am%d_%d", "an%d_%d")[k - 2] % (t, c), (("ll%d" % k, t, c),))
+                    V(n, lambda o=o, n=n, k=k, a3=a3, land=land: [vs(T.nk[:, 4 * o + k:4 * o + 4 * n:4], land[:, a3 + o:a3 + o + n], 4096.0 * (3 - k), None, A.add)],
+                      (("ll%d" % k, t, c),), (("nk", c, k),))
+                else:
+                    S(n, lambda q=q, o=o, n=n, k=k: [act(T.nk[:, 4 * o + k:4 * o + 4 * n:4], pslice(q, 0, n), F.Copy, bias=2048.0 + 4096.0 * (3 - k))], (), (("nk", c, k),), (q,))
+            V(n, lambda o=o, n=n, a3=a3, m1=m1: [vs(T.nk[:, 4 * o + 1:4 * o + 4 * n:4], m1[:, a3 + o:a3 + o + n], 8192.0, None, A.add)], ((m1k, t, c),), (("nk", c, 1),))
+            if c in rg and not hm:
+                b, m = CH[rg[c]][0], o + n - CH[rg[c]][0]
+                S(m, lambda b=b, m=m, a3=a3: [act(T.r4[:, 4 * b + 1:4 * b + 4 * m:4], T.lr1[:, a3 + b:a3 + b + m], F.Copy)], (("lr1", t, c),), [("r4", x, 1) for x in range(rg[c], c + 1)])
         for c in range(NC):
             o, n = chunk(c)
-            sl, rd = viewdiff(c, ENG2[c], "v2", T.l2, 0, T.xc, a3, T.y2, T.b2, (("l2", c),), ("xc", t), par)
+            sl, rd = viewdiff(c, ENG2[c], "v2", tab, v2, a3, xx, a3, T.y2, T.b2, ((k2, t, c),), xkey, T.xo, xbase)
             q = tile()
-            dist(c, q, sl, rd, lambda o=o, n=n, a3=a3: T.lr1[:, a3 + o:a3 + o + n], (("lr1", t, c),))
-            rests(2, c, q, lambda o=o, n=n: T.r4[:, 4 * o + 2:4 * o + 4 * n:4], (("r4", c, 2),))
+            if hm:
+                dist("v2", c, q, sl, rd, lambda o=o, n=n: T.r4[:, 4 * o + 1:4 * o + 4 * n:4], (("r4", c, 1),))
+            else:
+                dist("v2", c, q, sl, rd, lambda o=o, n=n, a3=a3: T.lr1[:, a3 + o:a3 + o + n], (("lr1", t, c),))
+            rests(2, c, q, lambda o=o, n=n: T.r4[:, 4 * o + 2:4 * o + 4 * n:4], (("r4", c, 2),), th, tk)
         for c in range(NC):
             o, n = chunk(c)
-            sl, rd = viewdiff(c, ENG3[c], "v3", T.l3, 0, T.xc, a3, T.y3, T.b3, (("l3", c),), ("xc", t), par)
+            sl, rd = viewdiff(c, ENG3[c], "v1", tab, v3, a3, xx, a3, T.y1, T.b1, ((k3, t, c),), xkey, T.xo, xbase)
             q = tile()
-            dist(c, q, sl, rd, lambda o=o, n=n: T.r4[:, 4 * o + 2:4 * o + 4 * n:4], (("r4", c, 2),))
-            rests(3, c, q, lambda o=o, n=n: T.r4[:, 4 * o + 3:4 * o + 4 * n:4], (("r4", c, 3),))
+            dist("v1", c, q, sl, rd, lambda o=o, n=n: T.r4[:, 4 * o + 2:4 * o + 4 * n:4], (("r4", c, 2),))
+            rests(3, c, q, lambda o=o, n=n: T.r4[:, 4 * o + 3:4 * o + 4 * n:4], (("r4", c, 3),), th, tk)
             V(4 * n, lambda o=o, n=n: [scan(T.es[:, 4 * o:4 * o + 4 * n], T.r4[:, 4 * o:4 * o + 4 * n], T.nk[:, 4 * o:4 * o + 4 * n], 0.0, A.min, A.max)],
               [("r4", c, k) for k in range(4)] + [("nk", c, k) for k in range(4)], (("es", c),))
-            V(n, lambda o=o, n=n: [vc(T.l4[:, o:o + n], T.es[:, 4 * o + 3:4 * o + 4 * n:4])], (("es", c),), (("l4", c),))
+            V(n, lambda o=o, n=n: [vc(T.ei[:, o:o + n], T.es[:, 4 * o + 3:4 * o + 4 * n:4])], (("es", c),), (("ei", c),))
+            V(n, lambda o=o, n=n: [vs(T.ef[:, o:o + n], T.ei[:, o:o + n], 4095, None, A.bitwise_and)], (("ei", c),), (("ef", c),))
+            V(n, lambda o=o, n=n: [vc(T.l4[:, o:o + n], T.ef[:, o:o + n])], (("ef", c),), (("l4", c),))
         if t == R - 1:
-            V(256, lambda: [vc(T.ei[:], T.es[:, 3:1024:4])], [("es", c) for c in range(NC)], ("ei",))
-            V(256, lambda: [vs(T.ef[:], T.ei[:], 4095, None, A.bitwise_and)], ("ei",), ("ef",))
-            V(256, lambda: [vc(T.yef[:], T.ef[:])], ("ef",), ("yef",))
-            send(home, ("yef",), T.yel[:], T.yef[:], "aye", ("yel",))
+            V(256, lambda: [vc(T.yef[:], T.ef[:])], [("ef", c) for c in range(NC)], ("yef",))
         for c in range(NC):
             o, n = chunk(c)
-            sl, rd = viewdiff(c, ENG4[c], "v4", T.l4, 0, T.xc, a3, T.y4, T.b4, (("l4", c), ("X4", 1), ("X4", 2), ("X4", 3)), ("xc", t), par, 16384)
+            sl, rd = viewdiff(c, ENG4[c], "v2", tab, T.l4, 0, xx, a3, T.y2, T.b2, (("l4", c),), xkey, T.xo, xbase)
             q = tile()
-            diag(c, T.y4, q, 0, (("v4", "y", c),))
+            diag(c, T.y2, q, 0, (("v2", "y", c),))
             if ENG4[c] == "S":
-                tasks[-1]["dur"] += 64 * PC
-                f0 = tasks[-1]["fn"]
-
-                def pf(q=q, o=o, n=n, a3=a3):
-                    r = [mm(pslice(q, 0, n), T.dg16[:, 128 * p:128 * p + 128], T.y4[:, 16 * o + p:16 * o + 16 * n:16], p == 0, False) for p in range(16)]
-                    return r + [mm(pslice(q, 0, n), T.idb[:], T.xc[:, a3 + o:a3 + o + n], False, True)]
+                def pf(q=q, o=o, n=n, a3=a3, xx=xx):
+                    r = [mm(pslice(q, 0, n), T.dg16[:, 128 * p:128 * p + 128], T.y2[:, 16 * o + p:16 * o + 16 * n:16], p == 0, False) for p in range(16)]
+                    return r + [mm(pslice(q, 0, n), T.idb[:], xx[:, a3 + o:a3 + o + n], False, True)]
                 tasks[-1]["fn"] = pf
             S(n, lambda q=q, o=o, n=n: [act(T.bb[:, o:o + n], pslice(q, 0, n), F.Sign, bias=-0.5)], (), (("bb", c),), (q,))
             q = tile()
-            dist(c, q, sl, rd)
+            dist("v2", c, q, sl, rd)
             S(n, lambda q=q, o=o, n=n: [act(T.val[:, o:o + n], pslice(q, 0, n), F.Identity, scale=-16.0, bias=T.vb[:])], ("vb",), (("val", c),), (q,))
             q = tile()
-            P(64, lambda q=q, o=o, n=n: [mm(pslice(q, 0, n), T.gt[:], T.bb[:, o:o + n], True, True)], ("gt", ("bb", c)), (), (q,))
+            P(64, lambda q=q, o=o, n=n, gm=gm, g0=g0: [mm(pslice(q, 0, n), gm[:, g0:g0 + 128], T.bb[:, o:o + n], True, True)], gk + (("bb", c),), (), (q,))
             S(n, lambda q=q, o=o, n=n: [act(T.sq[:, o:o + n], pslice(q, 0, n), F.Square)], (), (("sq", c),), (q,))
             q = tile()
-            P(128, lambda q=q, o=o, n=n: [mm(pslice(q, 0, n), T.ga[:], T.sq[:, o:o + n], True, False),
-                                          mm(pslice(q, 0, n), T.nga[:], T.one[:, 0:n], False, True)], ("ga", "nga", "one", ("sq", c)), (), (q,))
+            P(128, lambda q=q, o=o, n=n, gm=gm, g0=g0: [mm(pslice(q, 0, n), gm[:, g0 + 128:g0 + 256], T.sq[:, o:o + n], True, False),
+                                                        mm(pslice(q, 0, n), gm[:, g0 + 256:g0 + 384], T.one[:, 0:n], False, True)], gk + ("one", ("sq", c)), (), (q,))
             V(n, lambda q=q, o=o, n=n: [vt(T.key[:, o:o + n], pslice(q, 0, n), T.val[:, o:o + n], A.min)], (("val", c),), (("key", c),), (q,))
             q = tile()
             P(512, lambda q=q, o=o, n=n: [mm(pslice(q, 0, 128, n), T.key[:, o:o + n], T.i32[:], True, True)], (("key", c), "i32"), (), (q,))
@@ -348,43 +417,52 @@ def rank_program(g, core, T, topo):
             q = tile()
             P(4 * 64, lambda q=q, c=c, n=n: [mm(pslice(q, 0, n, 8), T.ks[0:n, 128 * c + 15:128 * c + 128:16], T.i32[0:n, 0:n], True, True)], (("ks", c), "i32"), (), (q,))
             S(n, lambda q=q, o=o, n=n: [act(T.mx[:, o:o + n], pslice(q, 0, n, 8), F.Copy)], (), (("mx", c),), (q,))
-            S(n + 150, lambda q=q, c=c, o=o, n=n: [act(T.cm[:, o:o + n], pslice(q, 0, n, 8), F.Sign, accum_out=T.cn[:, c:c + 1])], (), (("cn", c),), (q,))
             q = tile()
             P(4 * 64, lambda q=q, o=o, n=n: [mm(pslice(q, 0, n), T.ex[:], T.mx[:, o:o + n], True, True)], ("ex", ("mx", c)), (), (q,))
             V(n, lambda q=q, o=o, n=n: [vt(T.lt[:, o:o + n], pslice(q, 0, n), T.key[:, o:o + n], A.is_gt)], (("key", c),), (("lt", c),), (q,))
-            V(2 * n, lambda o=o, n=n, qb=qb: [vt(T.qg[:, qb + 2 * o + 1:qb + 2 * o + 2 * n:2], T.lt[:, o:o + n], T.key[:, o:o + n], A.min)], (("key", c), ("lt", c)), (("go", t, c),))
+            goc = T.go[:, o:o + n] if hm else T.qg[:, 2 * o + 1:2 * o + 2 * n:2]
+            guc = T.gu[:, o:o + n] if hm else T.qg[:, 2 * o:2 * o + 2 * n:2]
+            V(2 * n, lambda o=o, n=n, goc=goc: [vt(goc, T.lt[:, o:o + n], T.key[:, o:o + n], A.min)], (("key", c), ("lt", c)), (("go", t, c),))
             q = tile()
-            P(12 * n, lambda q=q, o=o, n=n, a3=a3: [mm(pslice(q, 0, n), T.i592[:], T.es[:, 4 * o + 3:4 * o + 4 * n:4], True, False),
-                                                    mm(pslice(q, 0, n), T.ni16[:], T.ec[:, a3 + o:a3 + o + n], False, False),
-                                                    mm(pslice(q, 0, n), T.ni32[:], T.val[:, o:o + n], False, True)],
-              ("i592", "ni16", "ni32", ("es", c), ("ec", t), ("val", c)), (), (q,))
-            V(n, lambda q=q, o=o, n=n, qb=qb: [vt(T.gu[:, o:o + n], pslice(q, 0, n), T.qg[:, qb + 2 * o + 1:qb + 2 * o + 2 * n:2], A.mult)],
-              (("go", t, c),), (("gu", c),), (q,))
-            q = tile()
-            P(8 * n, lambda q=q, o=o, n=n, a3=a3: [mm(pslice(q, 0, n), T.i32[:], T.gu[:, o:o + n], True, False),
-                                                   mm(pslice(q, 0, n), T.i16[:], T.ec[:, a3 + o:a3 + o + n], False, True)],
-              ("i32", "i16", ("gu", c), ("ec", t)), (), (q,))
-            S(n, lambda q=q, o=o, n=n, qb=qb: [act(T.qg[:, qb + 2 * o:qb + 2 * o + 2 * n:2], pslice(q, 0, n), F.Copy)], (), (("qs", t, c),), (q,))
+            P(12 * n, lambda q=q, o=o, n=n, a3=a3, ee=ee: [mm(pslice(q, 0, n), T.i592[:], T.es[:, 4 * o + 3:4 * o + 4 * n:4], True, False),
+                                                           mm(pslice(q, 0, n), T.ni16[:], ee[:, a3 + o:a3 + o + n], False, False),
+                                                           mm(pslice(q, 0, n), T.ni32[:], T.val[:, o:o + n], False, True)],
+              ("i592", "ni16", "ni32", ("es", c), eek, ("val", c)), (), (q,))
+            V(n, lambda q=q, n=n, goc=goc, guc=guc: [vt(guc, pslice(q, 0, n), goc, A.mult)], (("go", t, c),), (("gu", t, c),), (q,))
+            if hm:
+                if c == 0:
+                    wq = tile()
+                P(8 * n, lambda q=wq, o=o, n=n, a3=a3: [mm(pslice(q, o, n), T.i32[:], T.gu[:, o:o + n], True, False),
+                                                       mm(pslice(q, o, n), T.i16[:], T.eb[:, a3 + o:a3 + o + n], False, True)],
+                  ("i32", "i16", ("gu", t, c), ("eb", t)), (), (wq,))
             if c == NC - 1:
+                S(256, lambda: [act(T.cm[:], T.mx[:], F.Sign, accum_out=T.cn[:])], [("mx", x) for x in range(NC)], ("cn",))
                 q = tile()
-                P(256, lambda q=q: [mm(pslice(q, 0, NC), T.o16[:], T.cn[:], True, True)], ["o16"] + [("cn", x) for x in range(NC)], (), (q,))
-                V(64, lambda q=q, qb=qb: [g.vector.tensor_reduce(T.qg[:, qb + 512:qb + 513], pslice(q, 0, NC), AxisListType.X, A.add)], (), (("a16", t),), (q,))
-            if c in wg:
+                P(256, lambda q=q: [mm(pslice(q, 0, 1), T.o16[:], T.cn[:], True, True)], ("o16", "cn"), (), (q,))
+                a16 = T.a16[:] if hm else T.qg[:, 512:513]
+                V(64, lambda q=q, a16=a16: [vc(a16, pslice(q, 0, 1))], (), (("a16", t),), (q,))
+            if c in wg and not hm:
                 f = wg[c]
-                a, b = qb + 2 * CH[f][0], qb + 2 * o + 2 * n + (c == NC - 1)
-                send(home, [(k, t, x) for x in range(f, c + 1) for k in ("qs", "go")] + ([("a16", t)] if c == NC - 1 else []),
+                a, b = 2 * CH[f][0], 2 * o + 2 * n + (1 if c == NC - 1 else 0)
+                send(home, [(k, t, x) for x in range(f, c + 1) for k in ("gu", "go")] + ([("a16", t)] if c == NC - 1 else []),
                      T.ql[:, a:b], T.qg[:, a:b], "aw%d_%d" % (t, c), [("wl", t, x) for x in range(f, c + 1)])
         cur[0] = 0.0
-        V(256, lambda qb=qb: [vs(T.gaa[:], T.ql[:, qb + 1:qb + 512:2], T.ql[:, qb + 512:qb + 513], None, A.mult)], [("wl", t, c) for c in range(NC)], ("gaa",))
-        V(512, lambda qb=qb: [vt(T.wf[:], T.ql[:, qb:qb + 512:2], T.gaa[:], A.add)], ["gaa"], ("wf",))
+        if hm:
+            V(256, lambda: [vs(T.gaa[:], T.go[:], T.a16[:], None, A.mult)], [("a16", t)] + [("go", t, c) for c in range(NC)], ("gaa",))
+            V(256, lambda q=wq: [vt(T.wf[:], pslice(q, 0, 256), T.gaa[:], A.add)], ("gaa",), ("wf",), (wq,))
+        else:
+            wl = [("wl", t, c) for c in range(NC)]
+            S(256, lambda: [act(T.gaa[:], T.ql[:, 1:512:2], F.Copy, scale=T.ql[:, 512:513])], wl, ("gaa",))
+            V(512, lambda a3=a3: [vt(T.gu[:], T.ql[:, 0:512:2], T.eb16[:, a3:a3 + 256], A.add)], wl + [("eb16", t)], ("gu",))
+            V(512, lambda: [vt(T.wf[:], T.gu[:], T.gaa[:], A.add)], ("gaa", "gu"), ("wf",))
         if t < R - 1:
-            V(256, lambda t=t, a3=a3: [vs(T.dt[:, t:4096:16], T.wf[:], 4, 4095, A.arith_shift_right, A.bitwise_and)], ("wf",), ("D",))
+            V(256, lambda t=t: [vs(T.dt[:, t:4096:16], T.wf[:], 4, 4095, A.arith_shift_right, A.bitwise_and)], ("wf",), ("D",))
             V(256, lambda t=t, a3=a3: [vc(T.ydf[:, a3:a3 + 256], T.dt[:, t:4096:16])], ("D",), (("ydf", t),))
         else:
-            V(256, lambda: [vs(T.ei[:], T.wf[:], 4, 4095, A.arith_shift_right, A.bitwise_and)], ("wf",), ("ei",))
-            V(256, lambda a3=a3: [vc(T.ydf[:, a3:a3 + 256], T.ei[:])], ("ei",), (("ydf", t),))
+            V(256, lambda: [vs(T.wi[:], T.wf[:], 4, 4095, A.arith_shift_right, A.bitwise_and)], ("wf",), ("wi",))
+            V(256, lambda a3=a3: [vc(T.ydf[:, a3:a3 + 256], T.wi[:])], ("wi",), (("ydf", t),))
         load("Y", lambda a3=a3: g.sync.dma_start(T.yd[:, a3:a3 + 256], T.ydf[:, a3:a3 + 256]), 2.0, (("ydf", t),), (("yd", t),))
-    load("Y", lambda: g.sync.dma_start(T.ye[:], T.yel[:]), 2.0, ("yel",), ("ye",))
+    load("Y", lambda: g.sync.dma_start(T.ye[:], T.yef[:]), 2.0, ("yef",), ("ye",))
 
     n = len(tasks)
     succ = [[] for _ in range(n)]
@@ -397,7 +475,7 @@ def rank_program(g, core, T, topo):
     left = [len(tasks[i]["deps"]) for i in range(n)]
     ready_at, end = [0.0] * n, [0.0] * n
     ready = [i for i in range(n) if left[i] == 0]
-    free, owner, order, done = {}, [None] * 8, [], set()
+    free, owner, order, done = {}, [None] * 6, [], set()
 
     def bank_time(b):
         if owner[b] is None:
@@ -408,23 +486,24 @@ def rank_program(g, core, T, topo):
         return max(end[x] for x in u)
     while ready:
         best = None
-        bts = [(bank_time(b), b) for b in range(8)]
+        bts = [(bank_time(b), b) for b in range(6)]
         bts = [x for x in bts if x[0] is not None]
         for i in ready:
             tk = tasks[i]
             st = max(ready_at[i], free.get(tk["eng"], 0.0) if tk["eng"] != "R" else 0.0)
             nb = [q for q in tk["tl"] if tiles[q]["bank"] < 0]
             if nb:
-                if not bts:
+                ok = [x for x in bts if x[1] in tiles[nb[0]]["pool"]]
+                if not ok:
                     continue
-                st = max(st, min(bts)[0])
+                st = max(st, min(ok)[0])
             k = (round(st, 4), -rank[i] - tk["bias"], i)
             if best is None or k < best[0]:
                 best = (k, i, st, nb)
         _, i, st, nb = best
         tk = tasks[i]
         for q in nb:
-            b = min(bts)[1]
+            b = min(x for x in bts if x[1] in tiles[q]["pool"])[1]
             if owner[b] is not None:
                 tk["deps"] |= set(tiles[owner[b]]["users"])
             owner[b] = q

from concourse.mybir import AluOpType as A, ActivationFunctionType as F

SIZES = [112, 88, 56]
CH = [(sum(SIZES[:i]), n) for i, n in enumerate(SIZES)]
NC = len(CH)
R = 3
HM = [0, 1, 1]
ENG2, ENG3, ENG4 = "SSS", "RVS", "VVV"
LOW = [1, 0, 0]
WG, RG = [1, 1, 1], [1, 2]
BIAS = [0.5]
RK = ["S", "S", "V"]
SCRATCH = {
    "dt": ("sbuf", [128, 4096], "int32"), "xt": ("sbuf", [128, 4096], "bfloat16"),
    "thi": ("sbuf", [128, 1], "int32"), "tii": ("sbuf", [128, 3], "int32"), "sgi": ("sbuf", [128, 3], "int32"),
    "thf": ("sbuf", [128, 2], "float32"), "tif": ("sbuf", [128, 3], "float32"), "sgf": ("sbuf", [128, 3], "float32"),
    "pi": ("sbuf", [128, 1], "int32"), "pm": ("sbuf", [128, 1], "int32"), "pf": ("sbuf", [128, 1], "float32"),
    "pmf": ("sbuf", [128, 1], "float32"), "vb": ("sbuf", [128, 1], "float32"), "bse": ("sbuf", [128, 1], "float32"),
    "one": ("sbuf", [128, 128], "bfloat16"), "ob0": ("sbuf", [128, 128], "bfloat16"), "ob": ("sbuf", [128, 144], "bfloat16"),
    "ob2": ("sbuf", [128, 144], "bfloat16"), "obn": ("sbuf", [128, 144], "bfloat16"),
    "one32": ("sbuf", [128, 128], "float32"), "idb": ("sbuf", [128, 128], "bfloat16"), "i32": ("sbuf", [128, 128], "float32"),
    "ni32": ("sbuf", [128, 128], "float32"), "i592": ("sbuf", [128, 128], "float32"), "i16": ("sbuf", [128, 128], "float32"),
    "ni16": ("sbuf", [128, 128], "float32"), "dg16": ("sbuf", [128, 2048], "bfloat16"), "ex": ("sbuf", [8, 128], "float32"),
    "rs": ("sbuf", [128, 128], "float32"), "o16": ("sbuf", [8, 128], "float32"),
    "iom": ("sbuf", [128, 128], "float32"), "gk": ("sbuf", [128, 384], "float32"), "gs1": ("sbuf", [128, 128], "float32"),
    "gj": ("sbuf", [128, 128], "bfloat16"), "gm": ("sbuf", [128, 384], "bfloat16"), "gml": ("sbuf", [128, 1152], "bfloat16"),
    "thl": ("sbuf", [128, 6], "float32"),
    "le": ("sbuf", [128, 768], "uint16"), "eb": ("sbuf", [128, 768], "float32"), "eb16": ("sbuf", [128, 768], "float32"),
    "xn": ("sbuf", [128, 768], "bfloat16"), "xc": ("sbuf", [128, 768], "bfloat16"), "ec": ("sbuf", [128, 768], "float32"),
    "xo": ("sbuf", [128, 8192], "bfloat16"), "xs1": ("sbuf", [128, 4096], "bfloat16"), "xs2": ("sbuf", [128, 4096], "bfloat16"),
    "l1": ("sbuf", [128, 768], "uint16"), "ll1": ("sbuf", [128, 768], "uint16"),
    "l2": ("sbuf", [128, 768], "uint16"), "ll2": ("sbuf", [128, 768], "uint16"),
    "l3": ("sbuf", [128, 768], "uint16"), "ll3": ("sbuf", [128, 768], "uint16"), "l4": ("sbuf", [128, 256], "uint16"),
    "r1": ("sbuf", [128, 768], "bfloat16"), "lr1": ("sbuf", [128, 768], "bfloat16"),
    "g0": ("sbuf", [128, 4096], "float16"), "g1": ("sbuf", [128, 4096], "float16"),
    "y1": ("sbuf", [128, 4096], "bfloat16"), "y2": ("sbuf", [128, 4096], "bfloat16"),
    "b1": ("sbuf", [128, 4096], "bfloat16"), "b2": ("sbuf", [128, 4096], "bfloat16"),
    "nk": ("sbuf", [128, 1024], "float32"), "r4": ("sbuf", [128, 1024], "bfloat16"), "es": ("sbuf", [128, 1024], "float32"),
    "ei": ("sbuf", [128, 256], "int32"), "ef": ("sbuf", [128, 256], "int32"), "val": ("sbuf", [128, 256], "float32"),
    "bb": ("sbuf", [128, 256], "bfloat16"), "sq": ("sbuf", [128, 256], "bfloat16"), "key": ("sbuf", [128, 256], "float32"),
    "ks": ("sbuf", [128, 128 * NC], "float32"), "mx": ("sbuf", [8, 256], "float32"), "lt": ("sbuf", [128, 256], "bfloat16"),
    "cm": ("sbuf", [8, 256], "bfloat16"), "cn": ("sbuf", [8, 1], "float32"),
    "gu": ("sbuf", [128, 256], "float32"), "go": ("sbuf", [128, 256], "float32"), "a16": ("sbuf", [128, 1], "float32"),
    "gaa": ("sbuf", [128, 256], "float32"), "qg": ("sbuf", [128, 520], "float32"), "ql": ("sbuf", [128, 520], "float32"),
    "wf": ("sbuf", [128, 256], "int32"), "wi": ("sbuf", [128, 256], "int32"), "ydf": ("sbuf", [128, 768], "float32"), "yef": ("sbuf", [128, 256], "float32"),
}
for _i in range(4):
    SCRATCH["ps%d" % _i] = ("psum", [128, 512], "float32")
for _i in range(2):
    SCRATCH["ps%d" % (4 + _i)] = ("psum", [128, 1024], "float32")
SEMAPHORES = ["cv", "cs", "cp", "cg", "ls"]
SEMAPHORES += ["d%d" % i for i in range(20)]
for _t in range(R):
    SEMAPHORES += [x % _t for x in ("ax%d", "ae%d", "ag%d", "at%d")]
    SEMAPHORES += [x % (_t, _c) for x in ("al%d_%d", "ar%d_%d", "aw%d_%d", "am%d_%d", "an%d_%d") for _c in range(NC)]
SEMOF = {"V": "cv", "S": "cs", "P": "cp", "G": "cg"}
CY, GA, VF, SF, PC, HOP, CALL = 0.0009, 1.5, 0.13, 0.2, 0.00045, 2.8, 1.0


def rank_program(g, core, T, topo):
    me = T.rank_of(core)
    if me is None:
        return
    tasks, lastw, readers, tiles, sends, dmas, cur = [], {}, {}, [], [0], [0], [0.0]

    def add(eng, dur, fn, rd=(), wr=(), tl=(), after=(), lag=0.0):
        i = len(tasks)
        deps = set(after)
        for k in rd:
            if k in lastw:
                deps.add(lastw[k])
        for k in wr:
            if k in lastw:
                deps.add(lastw[k])
            deps |= readers.get(k, set())
        for q in tl:
            u = tiles[q]["users"]
            j = len(u) - 1
            while j >= 0 and tasks[u[j]]["eng"] == eng:
                j -= 1
            if j >= 0:
                e = tasks[u[j]]["eng"]
                while j >= 0 and tasks[u[j]]["eng"] == e:
                    deps.add(u[j])
                    j -= 1
            u.append(i)
        for k in rd:
            readers.setdefault(k, set()).add(i)
        for k in wr:
            lastw[k] = i
            readers[k] = set()
        deps.discard(i)
        tasks.append({"eng": eng, "dur": dur, "fn": fn, "deps": deps, "tl": list(tl), "lag": lag, "bias": cur[0]})
        return i

    def chunk(c):
        cur[0] = BIAS[0] * (NC - 1 - c)
        return CH[c]

    def tile(wide=False):
        tiles.append({"users": [], "bank": -1, "pool": (4, 5) if wide else (0, 1, 2, 3)})
        return len(tiles) - 1

    def pslice(q, a, n, P=128):
        return T["ps%d" % tiles[q]["bank"]][0:P, a:a + n]

    def V(n, fn, rd=(), wr=(), tl=()):
        return add("V", VF + CY * max(n, 64), fn, rd, wr, tl)

    def S(n, fn, rd=(), wr=(), tl=()):
        return add("S", SF + CY * max(n, 64), fn, rd, wr, tl)

    def P(n, fn, rd=(), wr=(), tl=()):
        return add("P", PC * n, fn, rd, wr, tl)

    def gq(n, fn, rd=(), wr=()):
        return add("G", 0.19 + 2 * CY * n, fn, rd, wr)

    def load(eng, fn, dur, rd=(), wr=()):
        k = dmas[0]
        dmas[0] += 1
        i = add("DMA" + eng, 0.1, fn, rd, wr, ())
        tasks[i]["sem"] = "d%d" % k
        j = add("R", 0.0, None, (), wr, (), after=(i,), lag=dur)
        tasks[j]["wait"] = ("d%d" % k, 16)

    def send(dst, src_key, out, in_, rsem, land_key, big=False, low=False):
        def pick(a, b):
            e = topo.engines(a, b)
            return e[len(e) // 2:] if big else e[:4] if low else e[:8]
        es = pick(core, dst)
        src = T.cores[(2 * me - T.rank_of(dst)) % 4]
        rid, pid, _ = topo.addr(dst)
        sends[0] += len(es)

        def fn():
            g.remote_dma(out, in_, T.sem[rsem], T.sem.ls, pid, rid, sum(1 << e for e in es))
            return []
        i = add("G", CALL, fn, src_key, (), ())
        j = add("R", 0.0, None, (), land_key, (), after=(i,), lag=14.0 if big else HOP)
        tasks[j]["wait"] = (rsem, len(pick(src, core)))

    mm = g.tensor.matmul
    vc, vt, vs = g.vector.tensor_copy, g.vector.tensor_tensor, g.vector.tensor_scalar
    scan = g.vector.tensor_tensor_scan
    act = g.scalar.activation

    cur[0] = 1000.0
    load("Y", lambda: g.sync.dma_start(T.tii[:], T.ti[:]), 3.0, (), ("tii",))
    load("Y", lambda: g.sync.dma_start(T.sgi[:], T.sg[:]), 3.0, (), ("sgi",))
    load("Y", lambda: g.sync.dma_start(T.thi[:], T.th[:]), 3.0, (), ("thi",))
    cur[0] = 0.0
    load("Y", lambda: g.sync.dma_start(T.dt[:], T.dg[:]), 8.0, (), ("D",))
    load("Y", lambda: g.sync.dma_start(T.xt[:], T.xv[:]), 10.5, (), ("X",))

    V(64, lambda: [g.vector.memset(T.one[:], 1.0)], (), ("one",))
    V(128, lambda: [g.vector.memset(T.one32[:], 1.0)], (), ("one32",))
    V(64, lambda: [g.vector.memset(T.ob[:], 0.0)], (), ("ob",))
    V(64, lambda: [g.vector.memset(T.o16[:], 16.0)], (), ("o16",))
    V(128, lambda: [g.vector.memset(T.rs[:], 1.0)], (), ("rs",))
    V(64, lambda: [g.vector.memset(T.rs[:, 0:128:16], 0.0)], (), ("rs",))
    V(1024, lambda: [g.vector.memset(T.dg16[:], 0.0)], (), ("dg16",))
    V(512, lambda: [g.vector.memset(T.r4[:], 0.0)], (), [("r4", c, k) for c in range(NC) for k in range(4)])
    gq(128, lambda: [g.affine_select(T.idb[:], T.one[:], [[-1, 128]], A.is_equal, 0.0, 0, 1)], ("one",), ("idb",))
    gq(128, lambda: [g.affine_select(T.ob0[:], T.one[:], [[0, 8], [1, 16]], A.is_equal, 0.0, 0, 0)], ("one",), ("ob0",))
    gq(128, lambda: [g.affine_select(T.ob0[:], T.ob0[:], [[-16, 8], [0, 16]], A.is_ge, 0.0, 0, 1)], ("ob0",), ("ob0",))
    gq(128, lambda: [g.affine_select(T.ob0[:], T.ob0[:], [[16, 8], [0, 16]], A.is_ge, 0.0, 15, -1)], ("ob0",), ("ob0",))
    gq(128, lambda: [g.affine_select(T.i32[:], T.one32[:], [[-1, 128]], A.is_equal, 0.0, 0, 1)], ("one32",), ("i32",))
    gq(128, lambda: [g.affine_select(T.ex[:], T.one32[0:8, :], [[-1, 8], [0, 16]], A.is_equal, 0.0, 0, 1)], ("one32",), ("ex",))
    gq(1, lambda: [g.iota(T.pi[:], [[1, 1]], 0, 1)], (), ("pi",))
    gq(128, lambda: [g.iota(T.iom[:], [[1, 128]], 0, 0, allow_small_or_imprecise_dtypes=True)], (), ("iom",))
    V(64, lambda: [vc(T.ob[:, 15:143], T.ob0[:])], ("ob0",), ("ob",))
    V(72, lambda: [vs(T.ob2[:], T.ob[:], 2.0, None, A.mult)], ("ob",), ("ob2",))
    V(72, lambda: [vs(T.obn[:], T.ob[:], -1.0, None, A.mult)], ("ob",), ("obn",))
    V(16 * 130, lambda: [vc(T.dg16[:, 129 * q:128 * q + 128:16], T.idb[:, q:128:16]) for q in range(16)], ("idb",), ("dg16",))
    for nm, v in (("i592", 592.0), ("i16", 16.0), ("ni16", -16.0), ("ni32", -1.0)):
        V(128, lambda nm=nm, v=v: [vs(T[nm][:], T.i32[:], v, None, A.mult)], ("i32",), (nm,))
    V(64, lambda: [vs(T.pm[:], T.pi[:], 15, None, A.bitwise_and)], ("pi",), ("pm",))
    V(64, lambda: [vc(T.pmf[:], T.pm[:])], ("pm",), ("pmf",))
    V(64, lambda: [vc(T.pf[:], T.pi[:])], ("pi",), ("pf",))
    V(64, lambda: [vt(T.bse[:], T.pf[:], T.pmf[:], A.subtract)], ("pf", "pmf"), ("bse",))
    V(64, lambda: [vs(T.vb[:], T.pmf[:], -1.0, 65536.0, A.mult, A.add)], ("pmf",), ("vb",))
    V(64, lambda: [vc(T.thf[:, 0:1], T.thi[:])], ("thi",), ("thf",))
    V(64, lambda: [vs(T.thf[:, 1:2], T.thi[:], -32768.0, 16384.0, A.mult, A.add)], ("thi",), ("thb",))
    V(64, lambda: [vc(T.sgf[:], T.sgi[:])], ("sgi",), ("sgf",))
    V(64, lambda: [vs(T.tif[:], T.tii[:], T.bse[:], None, A.add)], ("tii", "bse"), ("tif",))
    for k in range(3):
        V(128, lambda k=k: [vs(T.gk[:, 128 * k:128 * k + 128], T.iom[:], T.tif[:, k:k + 1], T.sgf[:, k:k + 1], A.is_equal, A.mult)],
          ("iom", "tif", "sgf"), (("gk", k),))
    V(256, lambda: [vt(T.gs1[:], T.gk[:, 0:128], T.gk[:, 128:256], A.add)], (("gk", 0), ("gk", 1)), ("gs1",))
    V(256, lambda: [vt(T.gj[:], T.gs1[:], T.gk[:, 256:384], A.add)], ("gs1", ("gk", 2)), ("gj",))
    S(128, lambda: [act(T.gm[:, 128:256], T.gj[:], F.Abs, scale=16384.0)], ("gj",), ("ga",))
    V(64, lambda: [vs(T.gm[:, 256:384], T.gm[:, 128:256], -1.0, None, A.mult)], ("ga",), ("nga",))
    q0 = tile()
    P(128, lambda: [mm(pslice(q0, 0, 128), T.gj[:], T.idb[:], True, True)], ("gj", "idb"), (), (q0,))
    S(128, lambda: [act(T.gm[:, 0:128], pslice(q0, 0, 128), F.Copy)], (), ("gt",), (q0,))

    for t in range(R):
        a, b = 256 * t, 256 * t + 256
        dst = T.cores[(me + 1 + t) % 4]
        V(256, lambda t=t, a=a, b=b: [vc(T.le[:, a:b], T.dt[:, t:4096:16])], ("D",), (("le", t),))
        V(256, lambda t=t, a=a, b=b: [vs(T.eb[:, a:b], T.dt[:, t:4096:16], 12288.0, None, A.add)], ("D",), (("eb", t),))
        S(256, lambda t=t, a=a, b=b: [act(T.xn[:, a:b], T.xt[:, t:4096:16], F.Copy, scale=-1.0)], ("X",), (("xn", t),))
        if not HM[t]:
            V(256, lambda a=a, b=b: [vs(T.eb16[:, a:b], T.eb[:, a:b], 16.0, None, A.mult)], (("eb", t),), (("eb16", t),))

    def tables(t, rd):
        dst = T.cores[(me - 1 - t) % 4]
        send(dst, ("X",) + rd, T["xs%d" % t][:], T.xt[:], "ax%d" % t, (("XS", t),), big=True)
        send(dst, ("ga", "nga", "gt") + rd, T.gml[:, 384 * t:384 * t + 384], T.gm[:], "ag%d" % t, (("gml", t),), low=True)
        send(dst, ("thf", "thb") + rd, T.thl[:, 2 * t:2 * t + 2], T.thf[:], "at%d" % t, (("thl", t),), low=True)

    def dgather(c, lst, lo, out, rd, wr):
        o, n = CH[c]
        V(16 * n * GA, lambda: [vs(out[:, 16 * o:16 * o + 16 * n], T.dt[:, 0:4096].indirect(lst[:, lo + o:lo + o + n]), -2048.0, None, A.add)],
          ("D",) + rd, wr)

    def diag(c, src, q, a, rd):
        o, n = CH[c]
        P(16 * max(n, 64), lambda: [mm(pslice(q, a, n), T.dg16[:, 128 * p:128 * p + 128], src[:, 16 * o + p:16 * o + 16 * n:16], p == 0, p == 15)
                                    for p in range(16)], rd + ("dg16",), (), (q,))

    def viewdiff(c, eng, name, tab, lst, lo, xneg, xo, yb, bb, rd, xkey, xrep, xbase):
        o, n = CH[c]
        w = 16 * n
        if eng == "S":
            S(w * GA, lambda: [act(yb[:, 16 * o:16 * o + w], tab[0][:, 0:4096].indirect(lst[:, lo + o:lo + o + n]), F.Copy)], tab[1] + rd, ((name, "y", c),))
            if xrep is not None:
                keys = []
                for a in range(0, w, 1024):
                    m = min(1024, w - a)
                    q = tile(True)

                    def pf(a=a, m=m, q=q):
                        r = []
                        for e in range(0, m, 512):
                            k = min(512, m - e)
                            i = 16 * o + a + e
                            r.append(mm(pslice(q, e, k), T.idb[:], yb[:, i:i + k], True, False))
                            r.append(mm(pslice(q, e, k), T.idb[:], xrep[:, xbase + i:xbase + i + k], False, True))
                        return r
                    P(2 * m, pf, ((name, "y", c), "idb") + xkey, (), (q,))
                    S(m, lambda a=a, m=m, q=q: [act(bb[:, 16 * o + a:16 * o + a + m], pslice(q, 0, m), F.Abs)], (), ((name, "b", c, a),), (q,))
                    keys.append((name, "b", c, a))
                return (lambda p: bb[:, 16 * o + p:16 * o + w:16], None), tuple(keys)
            pp = max(x for x in (1, 2, 4, 8, 16) if x * n <= 512)
            for h in range(16 // pp):
                q = tile(True)

                def pf(h=h, q=q):
                    r = []
                    for k in range(pp):
                        p = h * pp + k
                        r.append(mm(pslice(q, n * k, n), T.idb[:], yb[:, 16 * o + p:16 * o + w:16], True, False))
                        r.append(mm(pslice(q, n * k, n), T.idb[:], xneg[:, xo + o:xo + o + n], False, True))
                    return r
                P(2 * pp * max(n, 64), pf, ((name, "y", c), "idb") + xkey, (), (q,))
                S(pp * n, lambda h=h, q=q: [act(bb[:, 16 * o + h * pp * n:16 * o + (h + 1) * pp * n], pslice(q, 0, pp * n), F.Abs)], (), ((name, "b", c, h),), (q,))
            return (lambda p: bb[:, 16 * o + p * n:16 * o + (p + 1) * n], None), tuple((name, "b", c, h) for h in range(16 // pp))
        V(w * GA, lambda: [vt(yb[:, 16 * o:16 * o + w], tab[0][:, 0:4096].indirect(lst[:, lo + o:lo + o + n]), xrep[:, xbase + 16 * o:xbase + 16 * o + w], A.add)],
          tab[1] + xkey + rd, ((name, "y", c),))
        if eng == "R":
            V(w // 2, lambda: [vs(bb[:, 16 * o:16 * o + w], yb[:, 16 * o:16 * o + w], 0.0, None, A.max)], ((name, "y", c),), ((name, "b", c, 0),))
            return (lambda p: bb[:, 16 * o + p:16 * o + w:16], yb), ((name, "b", c, 0), (name, "y", c))
        S(w, lambda: [act(bb[:, 16 * o:16 * o + w], yb[:, 16 * o:16 * o + w], F.Abs)], ((name, "y", c),), ((name, "b", c, 0),))
        return (lambda p: bb[:, 16 * o + p:16 * o + w:16], None), ((name, "b", c, 0),)

    def dist(name, c, q, slices, rd, extra=None, xrd=()):
        o, n = CH[c]
        sl, rl = slices

        def pf():
            ob = T.ob if rl is None else T.ob2
            r = [mm(pslice(q, 0, n), ob[:, 15 - p:143 - p], sl(p), p == 0, p == 15 and extra is None and rl is None) for p in range(16)]
            if rl is not None:
                r += [mm(pslice(q, 0, n), T.obn[:, 15 - p:143 - p], rl[:, 16 * o + p:16 * o + 16 * n:16], False, p == 15 and extra is None) for p in range(16)]
            if extra is not None:
                r.append(mm(pslice(q, 0, n), T.idb[:], extra(), False, True))
            return r
        P((17 if rl is None else 33) * max(n, 64), pf, rd + ("ob", "ob2", "obn", "idb", (name, "y", c)) + xrd, (), (q,))

    def rests(k, c, q, out, wr, th, tk):
        n = CH[c][1]
        if RK[k - 1] == "V":
            V(n, lambda: [vs(out(), pslice(q, 0, n), th[0][:, th[1]:th[1] + 1], 16384.0, A.is_ge, A.mult)], tk, wr, (q,))
        else:
            S(n, lambda: [act(out(), pslice(q, 0, n), F.Relu, scale=32768.0, bias=th[0][:, th[1] + 1:th[1] + 2])], tk, wr, (q,))

    def repeat(out, ob, src, sb, rd, u):
        for p in range(16):
            gq(256, lambda p=p: [g.affine_select(out[:, ob + p:ob + 4096:16], src[:, sb:sb + 256], [[0, 256]], A.is_gt, 0.0, 1, 0)], rd, (("xo", u, p),))

    wg, rg = {}, {}
    for sizes, d in ((WG, wg), (RG, rg)):
        a = 0
        for x in sizes:
            d[a + x - 1] = a
            a += x
    for t in range(R):
        s = T.cores[(me + 1 + t) % 4]
        home = T.cores[(me - 1 - t) % 4]
        hm, par = HM[t], t % 2
        a3 = 256 * t
        own = ("thf", "thb")
        xown = tuple(("xo", par, p) for p in range(16))
        if hm:
            tab = (T["xs%d" % t], (("XS", t),))
            xx, xbase, xkey = T.xn, 4096 * par, xown
            ee, eek, th, tk = T.eb, ("eb", t), (T.thl, 2 * t), (("thl", t),)
            gm, g0, gk, m1, m1k = T.gml, 384 * t, (("gml", t),), T.l1, "l1"
            v2, v3, k2, k3 = T.ll2, T.ll3, "ll2", "ll3"
        else:
            tab = (T.xt, ("X",))
            xx, xbase, xkey = T.xc, 0, tuple(("xo", 0, p) for p in range(16))
            ee, eek, th, tk = T.ec, ("ec", t), (T.thf, 0), own
            gm, g0, gk, m1, m1k = T.gm, 0, ("ga", "nga", "gt"), T.ll1, "ll1"
            v2, v3, k2, k3 = T.l2, T.l3, "l2", "l3"
        for c in range(NC):
            o, n = chunk(c)
            dgather(c, T.le, a3, T.g0, (("le", t),), (("g0", c),))
            q = tile()
            diag(c, T.g0, q, 0, (("g0", c),))
            V(n, lambda q=q, o=o, n=n, a3=a3: [vs(T.l1[:, a3 + o:a3 + o + n], pslice(q, 0, n), 2048.0, None, A.add)], (), (("l1", t, c),), (q,))
            send(s, (("l1", t, c),), T.ll1[:, a3 + o:a3 + o + n], T.l1[:, a3 + o:a3 + o + n], "al%d_%d" % (t, c), (("ll1", t, c),), low=LOW[t])
        cur[0] = 0.0
        made = (("l1", t, NC - 1),)
        if not hm:
            send(s, (("xn", t),) + made, T.xc[:, a3:a3 + 256], T.xn[:, a3:a3 + 256], "ax%d" % t, (("xc", t),), low=LOW[t])
            send(s, (("eb", t),) + made, T.ec[:, a3:a3 + 256], T.eb[:, a3:a3 + 256], "ae%d" % t, (("ec", t),), low=LOW[t])
            repeat(T.xo, 0, T.xc, a3, (("xc", t),), 0)
        if t == 0:
            tables(1, made)
        gq(256, lambda a3=a3, ee=ee: [g.affine_select(T.nk[:, 0:1024:4], ee[:, a3:a3 + 256], [[0, 256]], A.is_gt, 0.0, 1, 0)], (eek,) + made, [("nk", c, 0) for c in range(NC)])
        if t < R - 1:
            u = (t + 1) % 2
            repeat(T.xo, 4096 * u, T.xn, a3 + 256, (("xn", t + 1),) + made, u)
        for c in range(NC):
            o, n = chunk(c)
            sl, rd = viewdiff(c, "S", "v1", (T.xt, ("X",)), T.l1, a3, T.xn, a3, T.y1, T.b1, (("l1", t, c),), xown if t else (("xn", t),), T.xo if t else None, 4096 * par)
            q = tile()
            dist("v1", c, q, sl, rd)
            if hm:
                rests(1, c, q, lambda o=o, n=n: T.r4[:, 4 * o + 1:4 * o + 4 * n:4], (("r4", c, 1),), (T.thf, 0), own)
            else:
                rests(1, c, q, lambda o=o, n=n, a3=a3: T.r1[:, a3 + o:a3 + o + n], (("r1", t, c),), (T.thf, 0), own)
            if c in rg and not hm:
                f = rg[c]
                a, b = a3 + CH[f][0], a3 + o + n
                send(s, [("r1", t, x) for x in range(f, c + 1)], T.lr1[:, a:b], T.r1[:, a:b], "ar%d_%d" % (t, c), [("lr1", t, x) for x in range(f, c + 1)], low=LOW[t])
        if t == 0:
            tables(2, (("lr1", 0, NC - 1),))
        for c in range(NC):
            o, n = chunk(c)
            for k, lst, lk, gb, gkey, lout in ((2, T.ll1, ("ll1", t, c), T.g1, ("g1", c), T.l2), (3, T.l2, ("l2", t, c), T.g0, ("g0", c), T.l3)):
                dgather(c, lst, a3, gb, (lk,), (gkey,))
                q = tile()
                diag(c, gb, q, 0, (gkey,))
                V(n, lambda q=q, o=o, n=n, lout=lout, a3=a3: [vs(lout[:, a3 + o:a3 + o + n], pslice(q, 0, n), 2048.0, None, A.add)], (), (("l%d" % k, t, c),), (q,))
                if hm:
                    land = (T.ll2, T.ll3)[k - 2]
                    send(home, (("l%d" % k, t, c),), land[:, a3 + o:a3 + o + n], lout[:, a3 + o:a3 + o + n], ("am%d_%d", "an%d_%d")[k - 2] % (t, c), (("ll%d" % k, t, c),))
                    V(n, lambda o=o, n=n, k=k, a3=a3, land=land: [vs(T.nk[:, 4 * o + k:4 * o + 4 * n:4], land[:, a3 + o:a3 + o + n], 4096.0 * (3 - k), None, A.add)],
                      (("ll%d" % k, t, c),), (("nk", c, k),))
                else:
                    S(n, lambda q=q, o=o, n=n, k=k: [act(T.nk[:, 4 * o + k:4 * o + 4 * n:4], pslice(q, 0, n), F.Copy, bias=2048.0 + 4096.0 * (3 - k))], (), (("nk", c, k),), (q,))
            V(n, lambda o=o, n=n, a3=a3, m1=m1: [vs(T.nk[:, 4 * o + 1:4 * o + 4 * n:4], m1[:, a3 + o:a3 + o + n], 8192.0, None, A.add)], ((m1k, t, c),), (("nk", c, 1),))
            if c in rg and not hm:
                b, m = CH[rg[c]][0], o + n - CH[rg[c]][0]
                S(m, lambda b=b, m=m, a3=a3: [act(T.r4[:, 4 * b + 1:4 * b + 4 * m:4], T.lr1[:, a3 + b:a3 + b + m], F.Copy)], (("lr1", t, c),), [("r4", x, 1) for x in range(rg[c], c + 1)])
        for c in range(NC):
            o, n = chunk(c)
            sl, rd = viewdiff(c, ENG2[c], "v2", tab, v2, a3, xx, a3, T.y2, T.b2, ((k2, t, c),), xkey, T.xo, xbase)
            q = tile()
            if hm:
                dist("v2", c, q, sl, rd, lambda o=o, n=n: T.r4[:, 4 * o + 1:4 * o + 4 * n:4], (("r4", c, 1),))
            else:
                dist("v2", c, q, sl, rd, lambda o=o, n=n, a3=a3: T.lr1[:, a3 + o:a3 + o + n], (("lr1", t, c),))
            rests(2, c, q, lambda o=o, n=n: T.r4[:, 4 * o + 2:4 * o + 4 * n:4], (("r4", c, 2),), th, tk)
        for c in range(NC):
            o, n = chunk(c)
            sl, rd = viewdiff(c, ENG3[c], "v1", tab, v3, a3, xx, a3, T.y1, T.b1, ((k3, t, c),), xkey, T.xo, xbase)
            q = tile()
            dist("v1", c, q, sl, rd, lambda o=o, n=n: T.r4[:, 4 * o + 2:4 * o + 4 * n:4], (("r4", c, 2),))
            rests(3, c, q, lambda o=o, n=n: T.r4[:, 4 * o + 3:4 * o + 4 * n:4], (("r4", c, 3),), th, tk)
            V(4 * n, lambda o=o, n=n: [scan(T.es[:, 4 * o:4 * o + 4 * n], T.r4[:, 4 * o:4 * o + 4 * n], T.nk[:, 4 * o:4 * o + 4 * n], 0.0, A.min, A.max)],
              [("r4", c, k) for k in range(4)] + [("nk", c, k) for k in range(4)], (("es", c),))
            V(n, lambda o=o, n=n: [vc(T.ei[:, o:o + n], T.es[:, 4 * o + 3:4 * o + 4 * n:4])], (("es", c),), (("ei", c),))
            V(n, lambda o=o, n=n: [vs(T.ef[:, o:o + n], T.ei[:, o:o + n], 4095, None, A.bitwise_and)], (("ei", c),), (("ef", c),))
            V(n, lambda o=o, n=n: [vc(T.l4[:, o:o + n], T.ef[:, o:o + n])], (("ef", c),), (("l4", c),))
        if t == R - 1:
            V(256, lambda: [vc(T.yef[:], T.ef[:])], [("ef", c) for c in range(NC)], ("yef",))
        for c in range(NC):
            o, n = chunk(c)
            sl, rd = viewdiff(c, ENG4[c], "v2", tab, T.l4, 0, xx, a3, T.y2, T.b2, (("l4", c),), xkey, T.xo, xbase)
            q = tile()
            diag(c, T.y2, q, 0, (("v2", "y", c),))
            if ENG4[c] == "S":
                def pf(q=q, o=o, n=n, a3=a3, xx=xx):
                    r = [mm(pslice(q, 0, n), T.dg16[:, 128 * p:128 * p + 128], T.y2[:, 16 * o + p:16 * o + 16 * n:16], p == 0, False) for p in range(16)]
                    return r + [mm(pslice(q, 0, n), T.idb[:], xx[:, a3 + o:a3 + o + n], False, True)]
                tasks[-1]["fn"] = pf
            S(n, lambda q=q, o=o, n=n: [act(T.bb[:, o:o + n], pslice(q, 0, n), F.Sign, bias=-0.5)], (), (("bb", c),), (q,))
            q = tile()
            dist("v2", c, q, sl, rd)
            S(n, lambda q=q, o=o, n=n: [act(T.val[:, o:o + n], pslice(q, 0, n), F.Identity, scale=-16.0, bias=T.vb[:])], ("vb",), (("val", c),), (q,))
            q = tile()
            P(64, lambda q=q, o=o, n=n, gm=gm, g0=g0: [mm(pslice(q, 0, n), gm[:, g0:g0 + 128], T.bb[:, o:o + n], True, True)], gk + (("bb", c),), (), (q,))
            S(n, lambda q=q, o=o, n=n: [act(T.sq[:, o:o + n], pslice(q, 0, n), F.Square)], (), (("sq", c),), (q,))
            q = tile()
            P(128, lambda q=q, o=o, n=n, gm=gm, g0=g0: [mm(pslice(q, 0, n), gm[:, g0 + 128:g0 + 256], T.sq[:, o:o + n], True, False),
                                                        mm(pslice(q, 0, n), gm[:, g0 + 256:g0 + 384], T.one[:, 0:n], False, True)], gk + ("one", ("sq", c)), (), (q,))
            V(n, lambda q=q, o=o, n=n: [vt(T.key[:, o:o + n], pslice(q, 0, n), T.val[:, o:o + n], A.min)], (("val", c),), (("key", c),), (q,))
            q = tile()
            P(512, lambda q=q, o=o, n=n: [mm(pslice(q, 0, 128, n), T.key[:, o:o + n], T.i32[:], True, True)], (("key", c), "i32"), (), (q,))
            V(128, lambda q=q, c=c, n=n: [scan(T.ks[0:n, 128 * c:128 * c + 128], T.rs[0:n, :], pslice(q, 0, 128, n), 0.0, A.mult, A.max)],
              ("rs",), (("ks", c),), (q,))
            q = tile()
            P(4 * 64, lambda q=q, c=c, n=n: [mm(pslice(q, 0, n, 8), T.ks[0:n, 128 * c + 15:128 * c + 128:16], T.i32[0:n, 0:n], True, True)], (("ks", c), "i32"), (), (q,))
            S(n, lambda q=q, o=o, n=n: [act(T.mx[:, o:o + n], pslice(q, 0, n, 8), F.Copy)], (), (("mx", c),), (q,))
            q = tile()
            P(4 * 64, lambda q=q, o=o, n=n: [mm(pslice(q, 0, n), T.ex[:], T.mx[:, o:o + n], True, True)], ("ex", ("mx", c)), (), (q,))
            V(n, lambda q=q, o=o, n=n: [vt(T.lt[:, o:o + n], pslice(q, 0, n), T.key[:, o:o + n], A.is_gt)], (("key", c),), (("lt", c),), (q,))
            goc = T.go[:, o:o + n] if hm else T.qg[:, 2 * o + 1:2 * o + 2 * n:2]
            guc = T.gu[:, o:o + n] if hm else T.qg[:, 2 * o:2 * o + 2 * n:2]
            V(2 * n, lambda o=o, n=n, goc=goc: [vt(goc, T.lt[:, o:o + n], T.key[:, o:o + n], A.min)], (("key", c), ("lt", c)), (("go", t, c),))
            q = tile()
            P(12 * n, lambda q=q, o=o, n=n, a3=a3, ee=ee: [mm(pslice(q, 0, n), T.i592[:], T.es[:, 4 * o + 3:4 * o + 4 * n:4], True, False),
                                                           mm(pslice(q, 0, n), T.ni16[:], ee[:, a3 + o:a3 + o + n], False, False),
                                                           mm(pslice(q, 0, n), T.ni32[:], T.val[:, o:o + n], False, True)],
              ("i592", "ni16", "ni32", ("es", c), eek, ("val", c)), (), (q,))
            V(n, lambda q=q, n=n, goc=goc, guc=guc: [vt(guc, pslice(q, 0, n), goc, A.mult)], (("go", t, c),), (("gu", t, c),), (q,))
            if hm:
                if c == 0:
                    wq = tile()
                P(8 * n, lambda q=wq, o=o, n=n, a3=a3: [mm(pslice(q, o, n), T.i32[:], T.gu[:, o:o + n], True, False),
                                                       mm(pslice(q, o, n), T.i16[:], T.eb[:, a3 + o:a3 + o + n], False, True)],
                  ("i32", "i16", ("gu", t, c), ("eb", t)), (), (wq,))
            if c == NC - 1:
                S(256, lambda: [act(T.cm[:], T.mx[:], F.Sign, accum_out=T.cn[:])], [("mx", x) for x in range(NC)], ("cn",))
                q = tile()
                P(256, lambda q=q: [mm(pslice(q, 0, 1), T.o16[:], T.cn[:], True, True)], ("o16", "cn"), (), (q,))
                a16 = T.a16[:] if hm else T.qg[:, 512:513]
                V(64, lambda q=q, a16=a16: [vc(a16, pslice(q, 0, 1))], (), (("a16", t),), (q,))
            if c in wg and not hm:
                f = wg[c]
                a, b = 2 * CH[f][0], 2 * o + 2 * n + (1 if c == NC - 1 else 0)
                send(home, [(k, t, x) for x in range(f, c + 1) for k in ("gu", "go")] + ([("a16", t)] if c == NC - 1 else []),
                     T.ql[:, a:b], T.qg[:, a:b], "aw%d_%d" % (t, c), [("wl", t, x) for x in range(f, c + 1)])
        cur[0] = 0.0
        if hm:
            V(256, lambda: [vs(T.gaa[:], T.go[:], T.a16[:], None, A.mult)], [("a16", t)] + [("go", t, c) for c in range(NC)], ("gaa",))
            V(256, lambda q=wq: [vt(T.wf[:], pslice(q, 0, 256), T.gaa[:], A.add)], ("gaa",), ("wf",), (wq,))
        else:
            wl = [("wl", t, c) for c in range(NC)]
            S(256, lambda: [act(T.gaa[:], T.ql[:, 1:512:2], F.Copy, scale=T.ql[:, 512:513])], wl, ("gaa",))
            V(512, lambda a3=a3: [vt(T.gu[:], T.ql[:, 0:512:2], T.eb16[:, a3:a3 + 256], A.add)], wl + [("eb16", t)], ("gu",))
            V(512, lambda: [vt(T.wf[:], T.gu[:], T.gaa[:], A.add)], ("gaa", "gu"), ("wf",))
        if t < R - 1:
            V(256, lambda t=t: [vs(T.dt[:, t:4096:16], T.wf[:], 4, 4095, A.arith_shift_right, A.bitwise_and)], ("wf",), ("D",))
            V(256, lambda t=t, a3=a3: [vc(T.ydf[:, a3:a3 + 256], T.dt[:, t:4096:16])], ("D",), (("ydf", t),))
        else:
            V(256, lambda: [vs(T.wi[:], T.wf[:], 4, 4095, A.arith_shift_right, A.bitwise_and)], ("wf",), ("wi",))
            V(256, lambda a3=a3: [vc(T.ydf[:, a3:a3 + 256], T.wi[:])], ("wi",), (("ydf", t),))
        load("Y", lambda a3=a3: g.sync.dma_start(T.yd[:, a3:a3 + 256], T.ydf[:, a3:a3 + 256]), 2.0, (("ydf", t),), (("yd", t),))
    load("Y", lambda: g.sync.dma_start(T.ye[:], T.yef[:]), 2.0, ("yef",), ("ye",))

    n = len(tasks)
    succ = [[] for _ in range(n)]
    for i in range(n):
        for d in tasks[i]["deps"]:
            succ[d].append(i)
    rank = [0.0] * n
    for i in range(n - 1, -1, -1):
        rank[i] = tasks[i]["dur"] + tasks[i]["lag"] + max([rank[j] for j in succ[i]] + [0.0])
    left = [len(tasks[i]["deps"]) for i in range(n)]
    ready_at, end = [0.0] * n, [0.0] * n
    ready = [i for i in range(n) if left[i] == 0]
    free, owner, order, done = {}, [None] * 6, [], set()

    def bank_time(b):
        if owner[b] is None:
            return 0.0
        u = tiles[owner[b]]["users"]
        if any(x not in done for x in u):
            return None
        return max(end[x] for x in u)
    while ready:
        best = None
        bts = [(bank_time(b), b) for b in range(6)]
        bts = [x for x in bts if x[0] is not None]
        for i in ready:
            tk = tasks[i]
            st = max(ready_at[i], free.get(tk["eng"], 0.0) if tk["eng"] != "R" else 0.0)
            nb = [q for q in tk["tl"] if tiles[q]["bank"] < 0]
            if nb:
                ok = [x for x in bts if x[1] in tiles[nb[0]]["pool"]]
                if not ok:
                    continue
                st = max(st, min(ok)[0])
            k = (round(st, 4), -rank[i] - tk["bias"], i)
            if best is None or k < best[0]:
                best = (k, i, st, nb)
        _, i, st, nb = best
        tk = tasks[i]
        for q in nb:
            b = min(x for x in bts if x[1] in tiles[q]["pool"])[1]
            if owner[b] is not None:
                tk["deps"] |= set(tiles[owner[b]]["users"])
            owner[b] = q
            tiles[q]["bank"] = b
        end[i] = st + tk["dur"] + tk["lag"]
        free[tk["eng"]] = st + tk["dur"]
        done.add(i)
        ready.remove(i)
        order.append(i)
        for j in succ[i]:
            left[j] -= 1
            ready_at[j] = max(ready_at[j], end[i])
            if left[j] == 0:
                ready.append(j)
    assert len(order) == n

    queue = {"V": g.vector, "S": g.scalar, "P": g.tensor, "G": g, "DMAY": g.sync, "DMAS": g.scalar}
    cnt = {"V": 0, "S": 0, "P": 0, "G": 0}
    know = {q: {} for q in ("V", "S", "P", "G", "DMAY")}
    fin = [None] * n
    for i in order:
        tk = tasks[i]
        if tk["eng"] == "R":
            fin[i] = (tk["wait"][0], tk["wait"][1], {tk["wait"][0]: tk["wait"][1]})
            continue
        kn = know["S" if tk["eng"] == "DMAS" else tk["eng"]]
        need = {}
        for d in tk["deps"]:
            if fin[d] is not None and need.get(fin[d][0], (0,))[0] < fin[d][1]:
                need[fin[d][0]] = fin[d][1:]
        for sname in sorted(need, key=lambda x: (-len(need[x][1]), x)):
            v, kk = need[sname]
            if kn.get(sname, 0) < v:
                queue[tk["eng"]].wait_ge(T.sem[sname], v)
                for x in kk:
                    if kn.get(x, 0) < kk[x]:
                        kn[x] = kk[x]
        calls = tk["fn"]()
        if tk["eng"] in cnt:
            sname = SEMOF[tk["eng"]]
            for x in calls:
                cnt[tk["eng"]] += 1
                x.then_inc(T.sem[sname], 1)
            if calls:
                kk = dict(kn)
                kk[sname] = cnt[tk["eng"]]
                fin[i] = (sname, cnt[tk["eng"]], kk)
        else:
            calls.then_inc(T.sem[tk["sem"]], 16)
    for e in cnt:
        g.wait_ge(T.sem[SEMOF[e]], cnt[e])
    g.wait_ge(T.sem.ls, sends[0])
    for k in range(dmas[0]):
        g.wait_ge(T.sem["d%d" % k], 16)
